import numpy as np
import ml_dtypes


def mxq(x, axis, fmt="e4m3"):
    dtype, down = {"e4m3": (ml_dtypes.float8_e4m3fn, 7), "e5m2": (ml_dtypes.float8_e5m2, 14)}[fmt]
    v = np.moveaxis(np.asarray(x, np.float32).astype(ml_dtypes.bfloat16).astype(np.float64), axis, -1)
    blocks = v.reshape(v.shape[:-1] + (-1, 32))
    amax = np.abs(blocks).max(-1, keepdims=True)
    byte = np.maximum(np.where(amax > 0, np.frexp(amax)[1] - 1 + 127, 0) - down, 1)
    scale = np.exp2(byte - 127.0)
    codes = (blocks / scale).astype(np.float32).astype(dtype).astype(np.float64)
    return np.moveaxis((codes * scale).reshape(v.shape), -1, axis)


WIDE = False


def mx_kscale(k):
    if not WIDE:
        return np.ones(k)
    levels = np.array([10, -10, 5, -5, 0])
    if k % 512:
        return np.exp2(np.random.permutation(np.resize(levels, k // 32))).repeat(32)
    a = np.empty((k // 512, 16))
    for p in range(k // 512):
        a[p, :8] = np.random.permutation(np.resize(levels, 8))
        for g in range(8):
            far = levels[np.abs(levels - a[p, g]) >= 10]
            a[p, g + 8] = far[np.random.randint(len(far))]
    return np.exp2(a.ravel()).repeat(32)


def f64(x):
    return np.asarray(x).astype(np.float64)


def striped(idx):
    return np.tile(idx.reshape(-1, 16).T, (8, 1)).astype(np.uint16)


def unstriped(offs):
    return offs[:16].T.reshape(-1).astype(np.int64)


E2M1 = np.array([0.0, 0.5, 1.0, 1.5, 2.0, 3.0, 4.0, 6.0, -0.0, -0.5, -1.0, -1.5, -2.0, -3.0, -4.0, -6.0])


def pack_weight(w, fmt):
    k, n = w.shape
    w = f64(np.asarray(w, np.float32).astype(ml_dtypes.bfloat16)).reshape(k // 32, 32, n)
    amax = np.abs(w).max(1)
    if fmt == "e4m3":
        byte = np.frexp(amax)[1] - 1 + 127 - 7
    else:
        mant, ex = np.frexp(amax / 6.0)
        byte = np.where(mant > 0.5, ex, ex - 1) + 127
    byte = np.clip(np.where(amax > 0, byte, 1), 1, 254)
    scaled = (w * np.exp2(127.0 - byte)[:, None, :]).reshape(k, n).astype(np.float32)
    by_word = np.ascontiguousarray(scaled.reshape(k // 512, 128, 4, n).transpose(0, 1, 3, 2))
    if fmt == "e4m3":
        words = by_word.astype(ml_dtypes.float8_e4m3fn).view(np.uint8)
    else:
        c = by_word.astype(ml_dtypes.float4_e2m1fn).view(np.uint8) & 0xF
        words = (c[..., 0::2] | (c[..., 1::2] << 4)).reshape(k // 512, 128, 2 * n)
    return np.ascontiguousarray(words), np.ascontiguousarray(byte.astype(np.uint8).reshape(k // 512, 16, n))


def unpack_weight(words, scales, fmt):
    g, _, n = scales.shape
    words = np.ascontiguousarray(words).reshape(g, 128, n, -1)
    if fmt == "e4m3":
        vals = words.view(ml_dtypes.float8_e4m3fn).astype(np.float64)
    else:
        nib = np.empty((g, 128, n, 4), np.uint8)
        nib[..., 0::2] = words & 0xF
        nib[..., 1::2] = words >> 4
        vals = E2M1[nib]
    vals = vals * np.repeat(np.exp2(scales.astype(np.float64) - 127.0), 8, axis=1)[..., None]
    return vals.transpose(0, 1, 3, 2).reshape(g * 512, n)


def gelu(v):
    return 0.5 * v * (1.0 + np.tanh(np.sqrt(2.0 / np.pi) * (v + 0.044715 * v**3)))


def striped8(idx):
    return np.concatenate([v.reshape(-1, 16).T for v in idx]).astype(np.uint16)


def unstriped8(offs):
    return np.stack([offs[16 * g:16 * g + 16].T.reshape(-1) for g in range(8)]).astype(np.int64)


def heads(h, wgt, idx8):
    r = np.arange(h.shape[0])
    return wgt[r // 4 % 128] * h[r[:, None], idx8[r % 512 // 64]]


T, S, P, K, H, N = 4096, 2048, 1024, 1024, 512, 768

def setup_inputs():
    n = np.random.standard_normal
    s = mx_kscale(K)[:, None]
    u = mx_kscale(H)[:, None]
    tab_words, tab_scales = pack_weight(n((K, T)) * s, "e4m3")
    offs = striped(np.random.permutation(T)[:S])
    w4_words, w4_scales = pack_weight(n((K, H)) / np.sqrt(K) / s, "e2m1")
    wg = (n((K, H)) / np.sqrt(K) / s).astype(np.float32)
    offs2 = striped8(np.stack([np.random.permutation(S)[:P] for _ in range(8)]))
    wgt = np.repeat(np.random.uniform(0.5, 2.0, (8, P)), 16, axis=0).astype(np.float32)
    site = (0.7 * n((H, P))).astype(np.float32)
    gain = (np.exp(0.3 * n(H)) * u[:, 0]).astype(np.float32)
    w8_words, w8_scales = pack_weight(n((H, N)) / np.sqrt(H) / u, "e4m3")
    return {"tab_words": tab_words, "tab_scales": tab_scales, "offs": offs,
            "w4_words": w4_words, "w4_scales": w4_scales, "wg": wg,
            "offs2": offs2, "wgt": wgt, "site": site, "gain": gain,
            "w8_words": w8_words, "w8_scales": w8_scales}

def reference(tab_words, tab_scales, offs, w4_words, w4_scales, wg, offs2, wgt, site, gain, w8_words, w8_scales):
    v = unpack_weight(tab_words, tab_scales, "e4m3")[:, unstriped(offs)]
    a = unpack_weight(w4_words, w4_scales, "e2m1").T @ v
    b = mxq(f64(wg), 0, "e4m3").T @ v
    h = a / (1.0 + np.exp(-b))
    x = heads(h, f64(wgt), unstriped8(offs2))
    z = np.tanh(x + f64(site)) * f64(gain)[:, None]
    return unpack_weight(w8_words, w8_scales, "e4m3").T @ mxq(z, 0, "e4m3")

@@ -1,0 +1,258 @@
+from contextlib import ExitStack
+
+import concourse.mybir as mybir
+
+T, S, M, K, H, N = 4096, 2048, 1024, 1024, 512, 768
+FLOPS = 2 * (2 * K * H * S + H * N * M)
+
+F32 = mybir.dt.float32
+BF16 = mybir.dt.bfloat16
+I32 = mybir.dt.int32
+U32 = mybir.dt.uint32
+U16 = mybir.dt.uint16
+U8 = mybir.dt.uint8
+FP8X4 = mybir.dt.float8_e4m3fn_x4
+FP4X4 = mybir.dt.float4_e2m1fn_x4
+ACT = mybir.ActivationFunctionType
+ALU = mybir.AluOpType
+
+P = 128
+PACK = 4
+PASSES = K // (P * PACK)
+BANK = 512
+CHUNKS = S // BANK
+SITES = 256
+SITE_CHUNKS = M // SITES
+LANES = 16
+SPLIT = 80
+
+
+def tile_list_syntax_edge_types_kernel(
+    tc, tab_words, tab_scales, offs, w4_words, w4_scales, wg, offs2, wgt, site, gain, w8_words, w8_scales, out
+):
+    nc = tc.nc
+    with ExitStack() as ctx:
+        lists = ctx.enter_context(tc.tile_pool(name="lists", bufs=1))
+        keep = ctx.enter_context(tc.tile_pool(name="keep", bufs=1))
+        ring = ctx.enter_context(tc.tile_pool(name="ring", bufs=4))
+        psum = ctx.enter_context(tc.psum_pool(name="psum", bufs=8))
+
+        tab_bytes = keep.tile([P, T], U8, name="tab_bytes", tag="small_window", align_bytes=64)
+        nc.sync.dma_start(
+            out=tab_bytes[0:32, :].bitcast(I32), in_=tab_scales.rearrange("a q t -> (a q) t").bitcast(I32)
+        )
+        nc.vector.memset(tab_bytes[32:64, :].bitcast(I32), 0)
+        nc.vector.memset(tab_bytes[64:128, :].bitcast(I32), 0)
+        idx = lists.tile([P, S // LANES], U16, name="idx")
+        nc.sync.dma_start(idx[:], offs)
+        w4_raw = keep.tile([P, PASSES, H], U16, name="w4_raw", align_bytes=64)
+        nc.sync.dma_start(
+            out=w4_raw[:].bitcast(I32), in_=w4_words.rearrange("a p c -> p a c").bitcast(I32)
+        )
+        idx2 = lists.tile([P, M // LANES], U16, name="idx2")
+        nc.sync.dma_start(idx2[:], offs2)
+        v_bytes = [keep.tile([P, S], U8, name="v_bytes%d" % a, align_bytes=64) for a in range(PASSES)]
+        for a in range(PASSES):
+            nc.vector.memset(v_bytes[a][:].bitcast(I32), 0)
+        tab = []
+        for a in range(PASSES):
+            words = keep.tile([P, T], I32, name="tab%d" % a, tag="window%d" % a, align_bytes=64)
+            nc.sync.dma_start(out=words[:], in_=tab_words[a].rearrange("p t i -> p (t i)").bitcast(I32))
+            tab.append(words)
+        wg_raw = []
+        for a in range(PASSES):
+            raw = keep.tile([P, PACK, H], F32, name="wg_raw%d" % a, tag="raw%d" % a, align_bytes=64)
+            nc.sync.dma_start(
+                out=raw[:], in_=wg[a * P * PACK : (a + 1) * P * PACK, :].rearrange("(p j) c -> p j c", j=PACK)
+            )
+            wg_raw.append(raw)
+
+        w4_bytes_raw = keep.tile([P, PASSES, H], U8, name="w4_bytes_raw", align_bytes=64)
+        nc.gpsimd.memset(w4_bytes_raw[:].rearrange("p a c -> p (a c)").bitcast(I32), 0)
+        for q in range(4):
+            nc.gpsimd.dma_start(
+                out=w4_bytes_raw[32 * q : 32 * q + 4, :, :].bitcast(I32),
+                in_=w4_scales[:, 4 * q : 4 * q + 4, :].rearrange("a r c -> r a c").bitcast(I32),
+            )
+        gains = keep.tile([P, PACK], F32, name="gains")
+        nc.gpsimd.dma_start(out=gains[:], in_=gain.rearrange("(p i) -> p i", i=PACK))
+
+        w4_codes = keep.tile([P, PASSES, H], U16, name="w4_codes", align_bytes=64)
+        nc.vector.tensor_copy(
+            out=w4_codes[:].rearrange("p a (i m) -> p a i m", i=PACK),
+            in_=w4_raw[:].rearrange("p a (m i) -> p a i m", i=PACK),
+        )
+
+        picked = keep.tile([P, S], U8, name="picked", align_bytes=64)
+        nc.vector.tensor_copy(out=picked[:], in_=tab_bytes[:].indirect(idx[:]))
+        for q in range(4):
+            for a in range(PASSES):
+                queue = nc.gpsimd if q == 3 else nc.scalar
+                queue.dma_start(
+                    out=v_bytes[a][32 * q : 32 * q + 4, :].bitcast(I32),
+                    in_=picked[16 * a + 4 * q : 16 * a + 4 * q + 4, :].bitcast(I32),
+                )
+        weights = keep.tile([P, M], F32, name="weights", tag="small_window", align_bytes=64)
+        nc.sync.dma_start(out=weights[:], in_=wgt)
+
+        w4_bytes = keep.tile([P, PASSES, H], U8, name="w4_bytes", align_bytes=64)
+        nc.vector.tensor_copy(
+            out=w4_bytes[:].rearrange("p a (i m) -> p a i m", i=PACK),
+            in_=w4_bytes_raw[:].rearrange("p a (m i) -> p a i m", i=PACK),
+        )
+
+        v0 = keep.tile([P, S], U32, name="v0", align_bytes=64)
+        nc.vector.tensor_copy(out=v0[:], in_=tab[0][:].bitcast(U32).indirect(idx[:]))
+        sites = keep.tile([P, PACK, M], F32, name="sites", tag="window0", align_bytes=64)
+        nc.sync.dma_start(out=sites[:], in_=site.rearrange("(p i) m -> p i m", i=PACK))
+
+        def rounded(a):
+            return keep.tile([P, PACK, P, PACK], BF16, name="wg_bf%d" % a, align_bytes=64)
+
+        def views(dst, a, lo, hi):
+            return (
+                dst[:].rearrange("p i m j -> p m i j")[:, lo:hi],
+                wg_raw[a][:].rearrange("p j (m i) -> p m i j", i=PACK)[:, lo:hi],
+            )
+
+        wg_bf = [rounded(a) for a in range(PASSES)]
+        dst, src = views(wg_bf[0], 0, 0, P)
+        nc.scalar.copy(out=dst, in_=src)
+
+        w8_bytes = keep.tile([P, N], U8, name="w8_bytes", tag="raw0", align_bytes=64)
+        nc.gpsimd.memset(w8_bytes[:].bitcast(I32), 0)
+        for q in range(4):
+            nc.sync.dma_start(
+                out=w8_bytes[32 * q : 32 * q + 4, :].bitcast(I32),
+                in_=w8_scales[0, 4 * q : 4 * q + 4, :].bitcast(I32),
+            )
+
+        v1 = []
+        cols = BANK // LANES
+        for c in range(CHUNKS):
+            piece = keep.tile([P, BANK], U32, name="v1_%d" % c, align_bytes=64)
+            nc.vector.tensor_copy(out=piece[:], in_=tab[1][:].bitcast(U32).indirect(idx[:, c * cols : (c + 1) * cols]))
+            v1.append(piece)
+        w8_codes = keep.tile([P, N], I32, name="w8_codes", tag="window1", align_bytes=64)
+        nc.sync.dma_start(out=w8_codes[:], in_=w8_words[0].rearrange("p c i -> p (c i)").bitcast(I32))
+
+        wg_codes = [keep.tile([P, H], U32, name="wg_codes%d" % a, align_bytes=64) for a in range(PASSES)]
+        wg_bytes = [keep.tile([P, H], U8, name="wg_bytes%d" % a, align_bytes=64) for a in range(PASSES)]
+
+        def quantize_wg(a):
+            nc.vector.quantize_mx(
+                out=wg_codes[a][:].bitcast(FP8X4),
+                scales=wg_bytes[a][:],
+                in_=wg_bf[a][:].rearrange("p i m j -> p (i m j)"),
+            )
+
+        dst, src = views(wg_bf[1], 1, SPLIT, P)
+        nc.scalar.copy(out=dst, in_=src)
+        dst, src = views(wg_bf[1], 1, 0, SPLIT)
+        nc.vector.tensor_copy(out=dst, in_=src)
+        quantize_wg(0)
+        quantize_wg(1)
+
+        def table(a, c):
+            span = slice(c * BANK, (c + 1) * BANK)
+            if a == 0:
+                return v0[:, span].bitcast(FP8X4), v_bytes[0][:, span]
+            return v1[c][:].bitcast(FP8X4), v_bytes[1][:, span]
+
+        def product(i, c, gate):
+            acc = psum.tile([P, BANK], F32, name="acc", tag="acc")
+            rows = slice(i * P, (i + 1) * P)
+            for a in range(PASSES):
+                codes, scales = table(a, c)
+                if gate:
+                    lhs, lhs_scale = wg_codes[a][:, rows].bitcast(FP8X4), wg_bytes[a][:, rows]
+                else:
+                    lhs, lhs_scale = w4_codes[:, a, rows].bitcast(FP4X4), w4_bytes[:, a, rows]
+                nc.tensor.matmul_mx(
+                    out=acc[:], lhsT=lhs, lhsT_scale=lhs_scale, rhs=codes, rhs_scale=scales,
+                    start=(a == 0), stop=(a == PASSES - 1),
+                )
+            return acc
+
+        h = [keep.tile([P, S], F32, name="h%d" % i) for i in range(PACK)]
+
+        def gated(i, c, content, gate):
+            sig = ring.tile([P, BANK], F32, name="sig")
+            nc.scalar.activation(out=sig[:], in_=gate[:], func=ACT.Sigmoid)
+            nc.vector.tensor_tensor(out=h[i][:, c * BANK : (c + 1) * BANK], in0=content[:], in1=sig[:], op=ALU.mult)
+
+        z = [keep.tile([P, 2, SITES, 2], BF16, name="z%d" % u, align_bytes=64) for u in range(SITE_CHUNKS)]
+
+        def pick(i, lo, hi):
+            x = keep.tile([P, hi - lo], F32, name="x%d_%d" % (i, lo))
+            nc.vector.tensor_tensor(
+                out=x[:], in0=h[i][:].indirect(idx2[:, lo // LANES : hi // LANES]), in1=weights[:, lo:hi], op=ALU.mult
+            )
+            return x
+
+        def add_site(x, i, lo, hi):
+            nc.vector.tensor_tensor(out=x[:], in0=x[:], in1=sites[:, i, lo:hi], op=ALU.add)
+
+        def squash(x, i, lo, hi):
+            nc.scalar.activation(out=x[:], in_=x[:], func=ACT.Tanh)
+            for u in range(lo // SITES, hi // SITES):
+                nc.scalar.activation(
+                    out=z[u][:, i // 2, :, i % 2], in_=x[:, u * SITES - lo : (u + 1) * SITES - lo], func=ACT.Copy,
+                    scale=gains[:, i : i + 1],
+                )
+
+        def close(u):
+            woven = ring.tile([P, SITES, PACK], BF16, name="woven", bufs=2, align_bytes=64)
+            nc.vector.tensor_copy(
+                out=woven[:].bitcast(F32), in_=z[u][:].rearrange("p a m e -> p a (m e)").bitcast(F32).rearrange("p a m -> p m a")
+            )
+            return woven
+
+        def scores(u, woven):
+            z_codes = ring.tile([P, SITES], U32, name="z_codes", bufs=2, align_bytes=64)
+            z_bytes = ring.tile([P, SITES], U8, name="z_bytes", bufs=2, align_bytes=64)
+            nc.vector.quantize_mx(
+                out=z_codes[:].bitcast(FP8X4), scales=z_bytes[:], in_=woven[:].rearrange("p m i -> p (m i)")
+            )
+            per_bank = BANK // SITES
+            for b in range(N // P // per_bank):
+                acc = psum.tile([P, per_bank, SITES], F32, name="acc2", tag="acc")
+                for e in range(per_bank):
+                    types = slice((b * per_bank + e) * P, (b * per_bank + e + 1) * P)
+                    nc.tensor.matmul_mx(
+                        out=acc[:, e, :], lhsT=w8_codes[:, types].bitcast(FP8X4), lhsT_scale=w8_bytes[:, types],
+                        rhs=z_codes[:].bitcast(FP8X4), rhs_scale=z_bytes[:], start=True, stop=True,
+                    )
+                result = ring.tile([P, per_bank, SITES], F32, name="result", bufs=6)
+                if b == 2 and u >= 2:
+                    nc.vector.tensor_copy(out=result[:], in_=acc[:])
+                else:
+                    nc.scalar.copy(out=result[:], in_=acc[:])
+                rows = out[b * per_bank * P : (b + 1) * per_bank * P, u * SITES : (u + 1) * SITES]
+                nc.sync.dma_start(out=rows.rearrange("(e p) m -> p e m", p=P), in_=result[:])
+
+        contents = [product(0, c, False) for c in range(CHUNKS)]
+        for c in range(CHUNKS):
+            gated(0, c, contents[c], product(0, c, True))
+        for i in range(1, PACK):
+            x = pick(i - 1, 0, M)
+            for c in range(CHUNKS):
+                content = product(i, c, False)
+                gated(i, c, content, product(i, c, True))
+                if c == 0:
+                    add_site(x, i - 1, 0, M)
+                    squash(x, i - 1, 0, M)
+        last = PACK - 1
+        xs = [None] * SITE_CHUNKS
+        woven = [None] * SITE_CHUNKS
+        for step in range(SITE_CHUNKS + 3):
+            if step < SITE_CHUNKS:
+                xs[step] = pick(last, step * SITES, (step + 1) * SITES)
+            if 0 <= step - 3 < SITE_CHUNKS:
+                scores(step - 3, woven[step - 3])
+            if 0 <= step - 2 < SITE_CHUNKS:
+                woven[step - 2] = close(step - 2)
+            if 0 <= step - 1 < SITE_CHUNKS:
+                u = step - 1
+                add_site(xs[u], last, u * SITES, (u + 1) * SITES)
+                squash(xs[u], last, u * SITES, (u + 1) * SITES)

@@ -24,7 +24,8 @@ CHUNKS = S // BANK
 SITES = 256
 SITE_CHUNKS = M // SITES
 LANES = 16
-SPLIT = 80
+PER_BANK = BANK // SITES
+EARLY = SITE_CHUNKS // 2
 
 
 def tile_list_syntax_edge_types_kernel(
@@ -34,6 +35,8 @@ def tile_list_syntax_edge_types_kernel(
     with ExitStack() as ctx:
         lists = ctx.enter_context(tc.tile_pool(name="lists", bufs=1))
         keep = ctx.enter_context(tc.tile_pool(name="keep", bufs=1))
+        shared = ctx.enter_context(tc.tile_pool(name="shared", bufs=1))
+        relay = ctx.enter_context(tc.tile_pool(name="relay", bufs=1))
         ring = ctx.enter_context(tc.tile_pool(name="ring", bufs=4))
         psum = ctx.enter_context(tc.psum_pool(name="psum", bufs=8))
 
@@ -41,31 +44,30 @@ def tile_list_syntax_edge_types_kernel(
         nc.sync.dma_start(
             out=tab_bytes[0:32, :].bitcast(I32), in_=tab_scales.rearrange("a q t -> (a q) t").bitcast(I32)
         )
-        nc.vector.memset(tab_bytes[32:64, :].bitcast(I32), 0)
+        nc.gpsimd.memset(tab_bytes[32:64, :].bitcast(I32), 0)
         nc.vector.memset(tab_bytes[64:128, :].bitcast(I32), 0)
         idx = lists.tile([P, S // LANES], U16, name="idx")
         nc.sync.dma_start(idx[:], offs)
+        tab = [
+            shared.tile([P, T], I32, name="tab0", offset=0, align_bytes=64),
+            keep.tile([P, T], I32, name="tab1", tag="window1", align_bytes=64),
+        ]
+        wg_raw = [keep.tile([P, PACK, H], F32, name="wg_raw%d" % a, tag="raw%d" % a, align_bytes=64) for a in range(PASSES)]
         w4_raw = keep.tile([P, PASSES, H], U16, name="w4_raw", align_bytes=64)
-        nc.sync.dma_start(
-            out=w4_raw[:].bitcast(I32), in_=w4_words.rearrange("a p c -> p a c").bitcast(I32)
-        )
+        for a in range(PASSES):
+            nc.sync.dma_start(out=tab[a][:], in_=tab_words[a].rearrange("p t i -> p (t i)").bitcast(I32))
+            if a == 0:
+                nc.sync.dma_start(
+                    out=w4_raw[:].bitcast(I32), in_=w4_words.rearrange("a p c -> p a c").bitcast(I32)
+                )
+            nc.sync.dma_start(
+                out=wg_raw[a][:], in_=wg[a * P * PACK : (a + 1) * P * PACK, :].rearrange("(p j) c -> p j c", j=PACK)
+            )
         idx2 = lists.tile([P, M // LANES], U16, name="idx2")
         nc.sync.dma_start(idx2[:], offs2)
         v_bytes = [keep.tile([P, S], U8, name="v_bytes%d" % a, align_bytes=64) for a in range(PASSES)]
         for a in range(PASSES):
             nc.vector.memset(v_bytes[a][:].bitcast(I32), 0)
-        tab = []
-        for a in range(PASSES):
-            words = keep.tile([P, T], I32, name="tab%d" % a, tag="window%d" % a, align_bytes=64)
-            nc.sync.dma_start(out=words[:], in_=tab_words[a].rearrange("p t i -> p (t i)").bitcast(I32))
-            tab.append(words)
-        wg_raw = []
-        for a in range(PASSES):
-            raw = keep.tile([P, PACK, H], F32, name="wg_raw%d" % a, tag="raw%d" % a, align_bytes=64)
-            nc.sync.dma_start(
-                out=raw[:], in_=wg[a * P * PACK : (a + 1) * P * PACK, :].rearrange("(p j) c -> p j c", j=PACK)
-            )
-            wg_raw.append(raw)
 
         w4_bytes_raw = keep.tile([P, PASSES, H], U8, name="w4_bytes_raw", align_bytes=64)
         nc.gpsimd.memset(w4_bytes_raw[:].rearrange("p a c -> p (a c)").bitcast(I32), 0)
@@ -77,37 +79,42 @@ def tile_list_syntax_edge_types_kernel(
         gains = keep.tile([P, PACK], F32, name="gains")
         nc.gpsimd.dma_start(out=gains[:], in_=gain.rearrange("(p i) -> p i", i=PACK))
 
-        w4_codes = keep.tile([P, PASSES, H], U16, name="w4_codes", align_bytes=64)
-        nc.vector.tensor_copy(
-            out=w4_codes[:].rearrange("p a (i m) -> p a i m", i=PACK),
-            in_=w4_raw[:].rearrange("p a (m i) -> p a i m", i=PACK),
-        )
 
         picked = keep.tile([P, S], U8, name="picked", align_bytes=64)
         nc.vector.tensor_copy(out=picked[:], in_=tab_bytes[:].indirect(idx[:]))
         for q in range(4):
             for a in range(PASSES):
-                queue = nc.gpsimd if q == 3 else nc.scalar
+                queue = nc.gpsimd if 2 * q + a >= 5 else nc.scalar
                 queue.dma_start(
                     out=v_bytes[a][32 * q : 32 * q + 4, :].bitcast(I32),
                     in_=picked[16 * a + 4 * q : 16 * a + 4 * q + 4, :].bitcast(I32),
                 )
-        weights = keep.tile([P, M], F32, name="weights", tag="small_window", align_bytes=64)
-        nc.sync.dma_start(out=weights[:], in_=wgt)
 
-        w4_bytes = keep.tile([P, PASSES, H], U8, name="w4_bytes", align_bytes=64)
+        cols = BANK // LANES
+
+        def look_up(a, c):
+            piece = keep.tile([P, BANK], U32, name="v%d_%d" % (a, c), tag="v%d_%d" % (a, c), align_bytes=64)
+            nc.vector.tensor_copy(out=piece[:], in_=tab[a][:].bitcast(U32).indirect(idx[:, c * cols : (c + 1) * cols]))
+            return piece
+
+        v0 = [look_up(0, c) for c in range(CHUNKS)]
+        w4_codes = shared.tile([P, PASSES, H], U16, name="w4_codes", offset=1024, align_bytes=64)
+        nc.vector.tensor_copy(
+            out=w4_codes[:].rearrange("p a (i m) -> p a i m", i=PACK),
+            in_=w4_raw[:].rearrange("p a (m i) -> p a i m", i=PACK),
+        )
+        w4_bytes = shared.tile([P, PASSES, H], U8, name="w4_bytes", offset=0, align_bytes=64)
         nc.vector.tensor_copy(
             out=w4_bytes[:].rearrange("p a (i m) -> p a i m", i=PACK),
             in_=w4_bytes_raw[:].rearrange("p a (m i) -> p a i m", i=PACK),
         )
-
-        v0 = keep.tile([P, S], U32, name="v0", align_bytes=64)
-        nc.vector.tensor_copy(out=v0[:], in_=tab[0][:].bitcast(U32).indirect(idx[:]))
-        sites = keep.tile([P, PACK, M], F32, name="sites", tag="window0", align_bytes=64)
+        weights = shared.tile([P, M], F32, name="weights", offset=3072, align_bytes=64)
+        nc.sync.dma_start(out=weights[:], in_=wgt)
+        sites = shared.tile([P, PACK, M], F32, name="sites", offset=7168, align_bytes=64)
         nc.sync.dma_start(out=sites[:], in_=site.rearrange("(p i) m -> p i m", i=PACK))
 
         def rounded(a):
-            return keep.tile([P, PACK, P, PACK], BF16, name="wg_bf%d" % a, align_bytes=64)
+            return keep.tile([P, PACK, P, PACK], BF16, name="wg_bf%d" % a, tag="v%d_3" % (2 - a), align_bytes=64)
 
         def views(dst, a, lo, hi):
             return (
@@ -127,15 +134,6 @@ def tile_list_syntax_edge_types_kernel(
                 in_=w8_scales[0, 4 * q : 4 * q + 4, :].bitcast(I32),
             )
 
-        v1 = []
-        cols = BANK // LANES
-        for c in range(CHUNKS):
-            piece = keep.tile([P, BANK], U32, name="v1_%d" % c, align_bytes=64)
-            nc.vector.tensor_copy(out=piece[:], in_=tab[1][:].bitcast(U32).indirect(idx[:, c * cols : (c + 1) * cols]))
-            v1.append(piece)
-        w8_codes = keep.tile([P, N], I32, name="w8_codes", tag="window1", align_bytes=64)
-        nc.sync.dma_start(out=w8_codes[:], in_=w8_words[0].rearrange("p c i -> p (c i)").bitcast(I32))
-
         wg_codes = [keep.tile([P, H], U32, name="wg_codes%d" % a, align_bytes=64) for a in range(PASSES)]
         wg_bytes = [keep.tile([P, H], U8, name="wg_bytes%d" % a, align_bytes=64) for a in range(PASSES)]
 
@@ -146,23 +144,29 @@ def tile_list_syntax_edge_types_kernel(
                 in_=wg_bf[a][:].rearrange("p i m j -> p (i m j)"),
             )
 
-        dst, src = views(wg_bf[1], 1, SPLIT, P)
-        nc.scalar.copy(out=dst, in_=src)
-        dst, src = views(wg_bf[1], 1, 0, SPLIT)
-        nc.vector.tensor_copy(out=dst, in_=src)
         quantize_wg(0)
+        v1 = [look_up(1, c) for c in range(CHUNKS - 1)]
+
+        dst, src = views(wg_bf[1], 1, 0, P // 2)
+        nc.scalar.copy(out=dst, in_=src)
+        dst, src = views(wg_bf[1], 1, P // 2, P)
+        nc.vector.tensor_copy(out=dst, in_=src)
         quantize_wg(1)
+        v1.append(look_up(1, CHUNKS - 1))
+        w8_codes = keep.tile([P, N], I32, name="w8_codes", tag="window1", align_bytes=64)
+        nc.sync.dma_start(out=w8_codes[:], in_=w8_words[0].rearrange("p c i -> p (c i)").bitcast(I32))
 
         def table(a, c):
             span = slice(c * BANK, (c + 1) * BANK)
             if a == 0:
-                return v0[:, span].bitcast(FP8X4), v_bytes[0][:, span]
+                return v0[c][:].bitcast(FP8X4), v_bytes[0][:, span]
             return v1[c][:].bitcast(FP8X4), v_bytes[1][:, span]
 
-        def product(i, c, gate):
-            acc = psum.tile([P, BANK], F32, name="acc", tag="acc")
+        def product(i, c, gate, acc=None, passes=range(PASSES)):
+            if acc is None:
+                acc = psum.tile([P, BANK], F32, name="acc", tag="acc")
             rows = slice(i * P, (i + 1) * P)
-            for a in range(PASSES):
+            for a in passes:
                 codes, scales = table(a, c)
                 if gate:
                     lhs, lhs_scale = wg_codes[a][:, rows].bitcast(FP8X4), wg_bytes[a][:, rows]
@@ -177,14 +181,24 @@ def tile_list_syntax_edge_types_kernel(
         h = [keep.tile([P, S], F32, name="h%d" % i) for i in range(PACK)]
 
         def gated(i, c, content, gate):
-            sig = ring.tile([P, BANK], F32, name="sig")
+            if i > 0 and c == CHUNKS - 1:
+                sig = relay.tile([P, BANK], F32, name="sig_last%d" % i, offset=(i - 1) * 4096 + 1024)
+            else:
+                sig = ring.tile([P, BANK], F32, name="sig")
             nc.scalar.activation(out=sig[:], in_=gate[:], func=ACT.Sigmoid)
             nc.vector.tensor_tensor(out=h[i][:, c * BANK : (c + 1) * BANK], in0=content[:], in1=sig[:], op=ALU.mult)
 
-        z = [keep.tile([P, 2, SITES, 2], BF16, name="z%d" % u, align_bytes=64) for u in range(SITE_CHUNKS)]
+        z = [keep.tile([P, 2, SITES, 2], BF16, name="z%d" % u, align_bytes=64) for u in range(EARLY)]
+
+        def pick_plain(i, lo, hi):
+            x = keep.tile([P, hi - lo], F32, name="x%d_%d" % (i, lo))
+            nc.vector.tensor_copy(out=x[:], in_=h[i][:].indirect(idx2[:, lo // LANES : hi // LANES]))
+            nc.gpsimd.tensor_tensor(out=x[:], in0=x[:], in1=weights[:, lo:hi], op=ALU.mult)
+            nc.gpsimd.tensor_tensor(out=x[:], in0=x[:], in1=sites[:, i, lo:hi], op=ALU.add)
+            return x
 
         def pick(i, lo, hi):
-            x = keep.tile([P, hi - lo], F32, name="x%d_%d" % (i, lo))
+            x = ring.tile([P, hi - lo], F32, name="x_last", bufs=3)
             nc.vector.tensor_tensor(
                 out=x[:], in0=h[i][:].indirect(idx2[:, lo // LANES : hi // LANES]), in1=weights[:, lo:hi], op=ALU.mult
             )
@@ -193,13 +207,20 @@ def tile_list_syntax_edge_types_kernel(
         def add_site(x, i, lo, hi):
             nc.vector.tensor_tensor(out=x[:], in0=x[:], in1=sites[:, i, lo:hi], op=ALU.add)
 
-        def squash(x, i, lo, hi):
+        def squash(x):
             nc.scalar.activation(out=x[:], in_=x[:], func=ACT.Tanh)
-            for u in range(lo // SITES, hi // SITES):
-                nc.scalar.activation(
-                    out=z[u][:, i // 2, :, i % 2], in_=x[:, u * SITES - lo : (u + 1) * SITES - lo], func=ACT.Copy,
-                    scale=gains[:, i : i + 1],
-                )
+
+        def squash_after(i, side, x):
+            t = relay.tile([P, BANK], F32, name="t%d_%d" % (i, side), offset=(i - 1) * 4096 + side * 2048)
+            nc.scalar.activation(out=t[:], in_=x[:], func=ACT.Tanh)
+            return t
+
+        def scale(u, i, t):
+            dst = z[u][:, i // 2, :, i % 2]
+            if u < EARLY:
+                nc.scalar.activation(out=dst, in_=t, func=ACT.Copy, scale=gains[:, i : i + 1])
+            else:
+                nc.vector.tensor_scalar(out=dst, in0=t, scalar1=gains[:, i : i + 1], scalar2=None, op0=ALU.mult)
 
         def close(u):
             woven = ring.tile([P, SITES, PACK], BF16, name="woven", bufs=2, align_bytes=64)
@@ -214,45 +235,70 @@ def tile_list_syntax_edge_types_kernel(
             nc.vector.quantize_mx(
                 out=z_codes[:].bitcast(FP8X4), scales=z_bytes[:], in_=woven[:].rearrange("p m i -> p (m i)")
             )
-            per_bank = BANK // SITES
-            for b in range(N // P // per_bank):
-                acc = psum.tile([P, per_bank, SITES], F32, name="acc2", tag="acc")
-                for e in range(per_bank):
-                    types = slice((b * per_bank + e) * P, (b * per_bank + e + 1) * P)
+            banks = []
+            for b in range(N // P // PER_BANK):
+                acc = psum.tile([P, PER_BANK, SITES], F32, name="acc2", tag="acc")
+                for e in range(PER_BANK):
+                    types = slice((b * PER_BANK + e) * P, (b * PER_BANK + e + 1) * P)
                     nc.tensor.matmul_mx(
                         out=acc[:, e, :], lhsT=w8_codes[:, types].bitcast(FP8X4), lhsT_scale=w8_bytes[:, types],
                         rhs=z_codes[:].bitcast(FP8X4), rhs_scale=z_bytes[:], start=True, stop=True,
                     )
-                result = ring.tile([P, per_bank, SITES], F32, name="result", bufs=6)
-                if b == 2 and u >= 2:
+                banks.append(acc)
+            return banks
+
+        def store(u, banks):
+            for b, acc in enumerate(banks):
+                result = ring.tile([P, PER_BANK, SITES], F32, name="result", bufs=8)
+                if (u, b) in ((3, 0), (3, 2)):
                     nc.vector.tensor_copy(out=result[:], in_=acc[:])
                 else:
                     nc.scalar.copy(out=result[:], in_=acc[:])
-                rows = out[b * per_bank * P : (b + 1) * per_bank * P, u * SITES : (u + 1) * SITES]
+                rows = out[b * PER_BANK * P : (b + 1) * PER_BANK * P, u * SITES : (u + 1) * SITES]
                 nc.sync.dma_start(out=rows.rearrange("(e p) m -> p e m", p=P), in_=result[:])
 
-        contents = [product(0, c, False) for c in range(CHUNKS)]
+        contents = [product(0, c, False, passes=[0]) for c in range(CHUNKS)]
+        gates = [product(0, c, True, passes=[0]) for c in range(CHUNKS)]
         for c in range(CHUNKS):
-            gated(0, c, contents[c], product(0, c, True))
+            product(0, c, False, contents[c], [1])
+        for c in range(CHUNKS):
+            gated(0, c, contents[c], product(0, c, True, gates[c], [1]))
+        last = PACK - 1
+        late = []
+        waiting = None
         for i in range(1, PACK):
-            x = pick(i - 1, 0, M)
+            early = pick_plain(i - 1, 0, BANK)
+            second = pick_plain(i - 1, BANK, M) if i < last else None
             for c in range(CHUNKS):
                 content = product(i, c, False)
                 gated(i, c, content, product(i, c, True))
-                if c == 0:
-                    add_site(x, i - 1, 0, M)
-                    squash(x, i - 1, 0, M)
-        last = PACK - 1
-        xs = [None] * SITE_CHUNKS
-        woven = [None] * SITE_CHUNKS
-        for step in range(SITE_CHUNKS + 3):
+            if waiting is not None:
+                late.append(squash_after(i, 0, waiting))
+            early = squash_after(i, 1, early)
+            for u in range(EARLY if i < last else 1):
+                scale(u, i - 1, early[:, u * SITES : (u + 1) * SITES])
+            waiting = second
+        for u in range(EARLY, SITE_CHUNKS):
+            z.append(keep.tile([P, 2, SITES, 2], BF16, name="z%d" % u, tag="v1_%d" % u, align_bytes=64))
+        banks = [None] * SITE_CHUNKS
+        for step in range(SITE_CHUNKS + 2):
+            picks = []
             if step < SITE_CHUNKS:
-                xs[step] = pick(last, step * SITES, (step + 1) * SITES)
-            if 0 <= step - 3 < SITE_CHUNKS:
-                scores(step - 3, woven[step - 3])
-            if 0 <= step - 2 < SITE_CHUNKS:
-                woven[step - 2] = close(step - 2)
+                for i in range(last if step < EARLY else last - 1, PACK):
+                    picks.append((i, pick(i, step * SITES, (step + 1) * SITES)))
+                for i, x in picks:
+                    add_site(x, i, step * SITES, (step + 1) * SITES)
+                    squash(x)
+                if step == 1:
+                    scale(1, last - 1, early[:, SITES : 2 * SITES])
+                if step < EARLY:
+                    scale(step, last, picks[0][1][:])
             if 0 <= step - 1 < SITE_CHUNKS:
-                u = step - 1
-                add_site(xs[u], last, u * SITES, (u + 1) * SITES)
-                squash(xs[u], last, u * SITES, (u + 1) * SITES)
+                banks[step - 1] = scores(step - 1, close(step - 1))
+            if EARLY <= step < SITE_CHUNKS:
+                for i in range(last - 1):
+                    scale(step, i, late[i][:, (step - EARLY) * SITES : (step - EARLY + 1) * SITES])
+                for i, x in picks:
+                    scale(step, i, x[:])
+            if 0 <= step - 2 < SITE_CHUNKS:
+                store(step - 2, banks[step - 2])

@@ -37,6 +37,7 @@ def tile_list_syntax_edge_types_kernel(
         keep = ctx.enter_context(tc.tile_pool(name="keep", bufs=1))
         shared = ctx.enter_context(tc.tile_pool(name="shared", bufs=1))
         relay = ctx.enter_context(tc.tile_pool(name="relay", bufs=1))
+        final = ctx.enter_context(tc.tile_pool(name="final", bufs=1))
         ring = ctx.enter_context(tc.tile_pool(name="ring", bufs=4))
         psum = ctx.enter_context(tc.psum_pool(name="psum", bufs=8))
 
@@ -97,7 +98,8 @@ def tile_list_syntax_edge_types_kernel(
             nc.vector.tensor_copy(out=piece[:], in_=tab[a][:].bitcast(U32).indirect(idx[:, c * cols : (c + 1) * cols]))
             return piece
 
-        v0 = [look_up(0, c) for c in range(CHUNKS)]
+        v0 = keep.tile([P, S], U32, name="v0", align_bytes=64)
+        nc.vector.tensor_copy(out=v0[:], in_=tab[0][:].bitcast(U32).indirect(idx[:]))
         w4_codes = shared.tile([P, PASSES, H], U16, name="w4_codes", offset=1024, align_bytes=64)
         nc.vector.tensor_copy(
             out=w4_codes[:].rearrange("p a (i m) -> p a i m", i=PACK),
@@ -150,7 +152,7 @@ def tile_list_syntax_edge_types_kernel(
         dst, src = views(wg_bf[1], 1, 0, P // 2)
         nc.scalar.copy(out=dst, in_=src)
         dst, src = views(wg_bf[1], 1, P // 2, P)
-        nc.vector.tensor_copy(out=dst, in_=src)
+        nc.gpsimd.tensor_scalar(out=dst, in0=src, scalar1=1.0, scalar2=0.0, op0=ALU.mult, op1=ALU.add)
         quantize_wg(1)
         v1.append(look_up(1, CHUNKS - 1))
         w8_codes = keep.tile([P, N], I32, name="w8_codes", tag="window1", align_bytes=64)
@@ -159,7 +161,7 @@ def tile_list_syntax_edge_types_kernel(
         def table(a, c):
             span = slice(c * BANK, (c + 1) * BANK)
             if a == 0:
-                return v0[c][:].bitcast(FP8X4), v_bytes[0][:, span]
+                return v0[:, span].bitcast(FP8X4), v_bytes[0][:, span]
             return v1[c][:].bitcast(FP8X4), v_bytes[1][:, span]
 
         def product(i, c, gate, acc=None, passes=range(PASSES)):
@@ -178,7 +180,8 @@ def tile_list_syntax_edge_types_kernel(
                 )
             return acc
 
-        h = [keep.tile([P, S], F32, name="h%d" % i) for i in range(PACK)]
+        h = [keep.tile([P, S], F32, name="h%d" % i) for i in range(PACK - 1)]
+        h.append(final.tile([P, S], F32, name="h_last", offset=0, align_bytes=64))
 
         def gated(i, c, content, gate):
             if i > 0 and c == CHUNKS - 1:
@@ -190,42 +193,31 @@ def tile_list_syntax_edge_types_kernel(
 
         z = [keep.tile([P, 2, SITES, 2], BF16, name="z%d" % u, align_bytes=64) for u in range(EARLY)]
 
-        def pick_plain(i, lo, hi):
-            x = keep.tile([P, hi - lo], F32, name="x%d_%d" % (i, lo))
-            nc.vector.tensor_copy(out=x[:], in_=h[i][:].indirect(idx2[:, lo // LANES : hi // LANES]))
-            nc.gpsimd.tensor_tensor(out=x[:], in0=x[:], in1=weights[:, lo:hi], op=ALU.mult)
-            nc.gpsimd.tensor_tensor(out=x[:], in0=x[:], in1=sites[:, i, lo:hi], op=ALU.add)
-            return x
-
-        def pick(i, lo, hi):
-            x = ring.tile([P, hi - lo], F32, name="x_last", bufs=3)
+        def pick(x, i, lo, hi):
             nc.vector.tensor_tensor(
-                out=x[:], in0=h[i][:].indirect(idx2[:, lo // LANES : hi // LANES]), in1=weights[:, lo:hi], op=ALU.mult
+                out=x, in0=h[i][:].indirect(idx2[:, lo // LANES : hi // LANES]), in1=weights[:, lo:hi], op=ALU.mult
             )
-            return x
 
-        def add_site(x, i, lo, hi):
-            nc.vector.tensor_tensor(out=x[:], in0=x[:], in1=sites[:, i, lo:hi], op=ALU.add)
-
-        def squash(x):
-            nc.scalar.activation(out=x[:], in_=x[:], func=ACT.Tanh)
+        def add_site(engine, x, i, lo, hi):
+            engine.tensor_tensor(out=x, in0=x, in1=sites[:, i, lo:hi], op=ALU.add)
 
         def squash_after(i, side, x):
             t = relay.tile([P, BANK], F32, name="t%d_%d" % (i, side), offset=(i - 1) * 4096 + side * 2048)
-            nc.scalar.activation(out=t[:], in_=x[:], func=ACT.Tanh)
+            nc.scalar.activation(out=t[:], in_=x, func=ACT.Tanh)
             return t
 
         def scale(u, i, t):
             dst = z[u][:, i // 2, :, i % 2]
-            if u < EARLY:
+            if i < 2:
                 nc.scalar.activation(out=dst, in_=t, func=ACT.Copy, scale=gains[:, i : i + 1])
             else:
                 nc.vector.tensor_scalar(out=dst, in0=t, scalar1=gains[:, i : i + 1], scalar2=None, op0=ALU.mult)
 
         def close(u):
             woven = ring.tile([P, SITES, PACK], BF16, name="woven", bufs=2, align_bytes=64)
+            pairs = z[u][:] if u < EARLY else z_late[:, :, (u - EARLY) * SITES : (u - EARLY + 1) * SITES, :]
             nc.vector.tensor_copy(
-                out=woven[:].bitcast(F32), in_=z[u][:].rearrange("p a m e -> p a (m e)").bitcast(F32).rearrange("p a m -> p m a")
+                out=woven[:].bitcast(F32), in_=pairs.rearrange("p a m e -> p a (m e)").bitcast(F32).rearrange("p a m -> p m a")
             )
             return woven
 
@@ -259,46 +251,55 @@ def tile_list_syntax_edge_types_kernel(
 
         contents = [product(0, c, False, passes=[0]) for c in range(CHUNKS)]
         gates = [product(0, c, True, passes=[0]) for c in range(CHUNKS)]
-        for c in range(CHUNKS):
+        for c in range(CHUNKS - 1):
             product(0, c, False, contents[c], [1])
         for c in range(CHUNKS):
+            if c == CHUNKS - 1:
+                product(0, c, False, contents[c], [1])
             gated(0, c, contents[c], product(0, c, True, gates[c], [1]))
         last = PACK - 1
         late = []
-        waiting = None
         for i in range(1, PACK):
-            early = pick_plain(i - 1, 0, BANK)
-            second = pick_plain(i - 1, BANK, M) if i < last else None
+            x = keep.tile([P, M], F32, name="x%d" % (i - 1))
+            pick(x[:], i - 1, 0, M)
+            add_site(nc.gpsimd, x[:], i - 1, 0, M)
             for c in range(CHUNKS):
                 content = product(i, c, False)
                 gated(i, c, content, product(i, c, True))
-            if waiting is not None:
-                late.append(squash_after(i, 0, waiting))
-            early = squash_after(i, 1, early)
-            for u in range(EARLY if i < last else 1):
+            early = squash_after(i, 0, x[:, 0:BANK])
+            for u in range(EARLY if i < last else 0):
                 scale(u, i - 1, early[:, u * SITES : (u + 1) * SITES])
-            waiting = second
-        for u in range(EARLY, SITE_CHUNKS):
-            z.append(keep.tile([P, 2, SITES, 2], BF16, name="z%d" % u, tag="v1_%d" % u, align_bytes=64))
+            late.append(squash_after(i, 1, x[:, BANK:M]))
+        z_late = final.tile([P, 2, BANK, 2], BF16, name="z_late", offset=0, align_bytes=64)
+
+        def scale_late(i, t, lo, hi):
+            nc.vector.tensor_scalar(
+                out=z_late[:, i // 2, lo:hi, i % 2], in0=t, scalar1=gains[:, i : i + 1], scalar2=None, op0=ALU.mult
+            )
+
         banks = [None] * SITE_CHUNKS
-        for step in range(SITE_CHUNKS + 2):
-            picks = []
+        picked_last = [None] * SITE_CHUNKS
+        for step in range(SITE_CHUNKS + 3):
+            lo, hi = step * SITES, (step + 1) * SITES
             if step < SITE_CHUNKS:
-                for i in range(last if step < EARLY else last - 1, PACK):
-                    picks.append((i, pick(i, step * SITES, (step + 1) * SITES)))
-                for i, x in picks:
-                    add_site(x, i, step * SITES, (step + 1) * SITES)
-                    squash(x)
-                if step == 1:
-                    scale(1, last - 1, early[:, SITES : 2 * SITES])
+                x = ring.tile([P, SITES], F32, name="x_last", bufs=2)
+                pick(x[:], last, lo, hi)
+                add_site(nc.vector, x[:], last, lo, hi)
+                nc.scalar.activation(out=x[:], in_=x[:], func=ACT.Tanh)
+                picked_last[step] = x
                 if step < EARLY:
-                    scale(step, last, picks[0][1][:])
-            if 0 <= step - 1 < SITE_CHUNKS:
+                    scale(step, last - 1, early[:, lo:hi])
+                    scale(step, last, x[:])
+            if 1 <= step <= EARLY:
                 banks[step - 1] = scores(step - 1, close(step - 1))
-            if EARLY <= step < SITE_CHUNKS:
-                for i in range(last - 1):
-                    scale(step, i, late[i][:, (step - EARLY) * SITES : (step - EARLY + 1) * SITES])
-                for i, x in picks:
-                    scale(step, i, x[:])
-            if 0 <= step - 2 < SITE_CHUNKS:
+            if step == SITE_CHUNKS - 1:
+                for i in range(last):
+                    scale_late(i, late[i][:], 0, BANK)
+                for u in range(EARLY, SITE_CHUNKS):
+                    scale_late(last, picked_last[u][:], (u - EARLY) * SITES, (u - EARLY + 1) * SITES)
+            if EARLY <= step - 2 < SITE_CHUNKS:
+                banks[step - 2] = scores(step - 2, close(step - 2))
+            if step in (2, 3):
                 store(step - 2, banks[step - 2])
+            if step - 3 >= EARLY:
+                store(step - 3, banks[step - 3])

@@ -25,7 +25,7 @@ SITES = 256
 SITE_CHUNKS = M // SITES
 LANES = 16
 PER_BANK = BANK // SITES
-EARLY = SITE_CHUNKS // 2
+SPLIT = 80
 
 
 def tile_list_syntax_edge_types_kernel(
@@ -36,12 +36,15 @@ def tile_list_syntax_edge_types_kernel(
         lists = ctx.enter_context(tc.tile_pool(name="lists", bufs=1))
         keep = ctx.enter_context(tc.tile_pool(name="keep", bufs=1))
         shared = ctx.enter_context(tc.tile_pool(name="shared", bufs=1))
+        early = ctx.enter_context(tc.tile_pool(name="early", bufs=1))
+        tail = ctx.enter_context(tc.tile_pool(name="tail", bufs=1))
         relay = ctx.enter_context(tc.tile_pool(name="relay", bufs=1))
-        final = ctx.enter_context(tc.tile_pool(name="final", bufs=1))
         ring = ctx.enter_context(tc.tile_pool(name="ring", bufs=4))
-        psum = ctx.enter_context(tc.psum_pool(name="psum", bufs=8))
+        psum = ctx.enter_context(tc.psum_pool(name="psum", bufs=4))
 
-        tab_bytes = keep.tile([P, T], U8, name="tab_bytes", tag="small_window", align_bytes=64)
+        w4_bytes_raw = keep.tile([P, PASSES, H], U8, name="w4_bytes_raw", align_bytes=64)
+        nc.gpsimd.memset(w4_bytes_raw[:].rearrange("p a c -> p (a c)").bitcast(I32), 0)
+        tab_bytes = keep.tile([P, T], U8, name="tab_bytes", align_bytes=64)
         nc.sync.dma_start(
             out=tab_bytes[0:32, :].bitcast(I32), in_=tab_scales.rearrange("a q t -> (a q) t").bitcast(I32)
         )
@@ -49,86 +52,85 @@ def tile_list_syntax_edge_types_kernel(
         nc.vector.memset(tab_bytes[64:128, :].bitcast(I32), 0)
         idx = lists.tile([P, S // LANES], U16, name="idx")
         nc.sync.dma_start(idx[:], offs)
+        for q in range(4):
+            nc.sync.dma_start(
+                out=w4_bytes_raw[32 * q : 32 * q + 4, :, :].bitcast(I32),
+                in_=w4_scales[:, 4 * q : 4 * q + 4, :].rearrange("a r c -> r a c").bitcast(I32),
+            )
+        w4_raw = early.tile([P, PASSES, H], U16, name="w4_raw", offset=19456, align_bytes=64)
+        nc.sync.dma_start(out=w4_raw[:].bitcast(I32), in_=w4_words.rearrange("a p c -> p a c").bitcast(I32))
         tab = [
             shared.tile([P, T], I32, name="tab0", offset=0, align_bytes=64),
             keep.tile([P, T], I32, name="tab1", tag="window1", align_bytes=64),
         ]
-        wg_raw = [keep.tile([P, PACK, H], F32, name="wg_raw%d" % a, tag="raw%d" % a, align_bytes=64) for a in range(PASSES)]
-        w4_raw = keep.tile([P, PASSES, H], U16, name="w4_raw", align_bytes=64)
         for a in range(PASSES):
             nc.sync.dma_start(out=tab[a][:], in_=tab_words[a].rearrange("p t i -> p (t i)").bitcast(I32))
-            if a == 0:
-                nc.sync.dma_start(
-                    out=w4_raw[:].bitcast(I32), in_=w4_words.rearrange("a p c -> p a c").bitcast(I32)
-                )
-            nc.sync.dma_start(
-                out=wg_raw[a][:], in_=wg[a * P * PACK : (a + 1) * P * PACK, :].rearrange("(p j) c -> p j c", j=PACK)
-            )
         idx2 = lists.tile([P, M // LANES], U16, name="idx2")
         nc.sync.dma_start(idx2[:], offs2)
         v_bytes = [keep.tile([P, S], U8, name="v_bytes%d" % a, align_bytes=64) for a in range(PASSES)]
-        for a in range(PASSES):
-            nc.vector.memset(v_bytes[a][:].bitcast(I32), 0)
+        nc.vector.memset(v_bytes[0][:].bitcast(I32), 0)
+        nc.gpsimd.memset(v_bytes[1][:].bitcast(I32), 0)
 
-        w4_bytes_raw = keep.tile([P, PASSES, H], U8, name="w4_bytes_raw", align_bytes=64)
-        nc.gpsimd.memset(w4_bytes_raw[:].rearrange("p a c -> p (a c)").bitcast(I32), 0)
-        for q in range(4):
-            nc.gpsimd.dma_start(
-                out=w4_bytes_raw[32 * q : 32 * q + 4, :, :].bitcast(I32),
-                in_=w4_scales[:, 4 * q : 4 * q + 4, :].rearrange("a r c -> r a c").bitcast(I32),
-            )
         gains = keep.tile([P, PACK], F32, name="gains")
         nc.gpsimd.dma_start(out=gains[:], in_=gain.rearrange("(p i) -> p i", i=PACK))
 
-
         picked = keep.tile([P, S], U8, name="picked", align_bytes=64)
         nc.vector.tensor_copy(out=picked[:], in_=tab_bytes[:].indirect(idx[:]))
-        for q in range(4):
-            for a in range(PASSES):
-                queue = nc.gpsimd if 2 * q + a >= 5 else nc.scalar
-                queue.dma_start(
+
+        def move_scales(a):
+            for q in range(4):
+                nc.sync.dma_start(
                     out=v_bytes[a][32 * q : 32 * q + 4, :].bitcast(I32),
                     in_=picked[16 * a + 4 * q : 16 * a + 4 * q + 4, :].bitcast(I32),
                 )
 
-        cols = BANK // LANES
-
-        def look_up(a, c):
-            piece = keep.tile([P, BANK], U32, name="v%d_%d" % (a, c), tag="v%d_%d" % (a, c), align_bytes=64)
-            nc.vector.tensor_copy(out=piece[:], in_=tab[a][:].bitcast(U32).indirect(idx[:, c * cols : (c + 1) * cols]))
-            return piece
-
-        v0 = keep.tile([P, S], U32, name="v0", align_bytes=64)
-        nc.vector.tensor_copy(out=v0[:], in_=tab[0][:].bitcast(U32).indirect(idx[:]))
-        w4_codes = shared.tile([P, PASSES, H], U16, name="w4_codes", offset=1024, align_bytes=64)
+        move_scales(0)
+        w4_codes = keep.tile([P, PASSES, H], U16, name="w4_codes", align_bytes=64)
         nc.vector.tensor_copy(
             out=w4_codes[:].rearrange("p a (i m) -> p a i m", i=PACK),
             in_=w4_raw[:].rearrange("p a (m i) -> p a i m", i=PACK),
         )
-        w4_bytes = shared.tile([P, PASSES, H], U8, name="w4_bytes", offset=0, align_bytes=64)
+        wg_raw = [early.tile([P, PACK, H], F32, name="wg_raw%d" % a, offset=12288 + 8192 * a, align_bytes=64) for a in range(PASSES)]
+        for a in range(PASSES):
+            nc.sync.dma_start(
+                out=wg_raw[a][:], in_=wg[a * P * PACK : (a + 1) * P * PACK, :].rearrange("(p j) c -> p j c", j=PACK)
+            )
+            if a == 0:
+                move_scales(1)
+
+        cols = BANK // LANES
+
+        def look_up(c):
+            piece = keep.tile([P, BANK], U32, name="v1_%d" % c, tag="v1_%d" % c, align_bytes=64)
+            nc.vector.tensor_copy(out=piece[:], in_=tab[1][:].bitcast(U32).indirect(idx[:, c * cols : (c + 1) * cols]))
+            return piece
+
+        v0 = keep.tile([P, S], U32, name="v0", align_bytes=64)
+        nc.vector.tensor_copy(out=v0[:], in_=tab[0][:].bitcast(U32).indirect(idx[:]))
+        w4_bytes = keep.tile([P, PASSES, H], U8, name="w4_bytes", align_bytes=64)
         nc.vector.tensor_copy(
             out=w4_bytes[:].rearrange("p a (i m) -> p a i m", i=PACK),
             in_=w4_bytes_raw[:].rearrange("p a (m i) -> p a i m", i=PACK),
         )
-        weights = shared.tile([P, M], F32, name="weights", offset=3072, align_bytes=64)
-        nc.sync.dma_start(out=weights[:], in_=wgt)
-        sites = shared.tile([P, PACK, M], F32, name="sites", offset=7168, align_bytes=64)
-        nc.sync.dma_start(out=sites[:], in_=site.rearrange("(p i) m -> p i m", i=PACK))
+        v1 = [look_up(c) for c in range(CHUNKS)]
 
-        def rounded(a):
-            return keep.tile([P, PACK, P, PACK], BF16, name="wg_bf%d" % a, tag="v%d_3" % (2 - a), align_bytes=64)
-
-        def views(dst, a, lo, hi):
-            return (
-                dst[:].rearrange("p i m j -> p m i j")[:, lo:hi],
-                wg_raw[a][:].rearrange("p j (m i) -> p m i j", i=PACK)[:, lo:hi],
+        def round_wg(a):
+            dst = keep.tile([P, PACK, P, PACK], BF16, name="wg_bf%d" % a, align_bytes=64)
+            o = dst[:].rearrange("p i m j -> p m i j")
+            s = wg_raw[a][:].rearrange("p j (m i) -> p m i j", i=PACK)
+            nc.scalar.copy(out=o[:, :SPLIT], in_=s[:, :SPLIT])
+            nc.gpsimd.tensor_scalar(
+                out=o[:, SPLIT:], in0=s[:, SPLIT:], scalar1=1.0, scalar2=0.0, op0=ALU.mult, op1=ALU.add
             )
+            return dst
 
-        wg_bf = [rounded(a) for a in range(PASSES)]
-        dst, src = views(wg_bf[0], 0, 0, P)
-        nc.scalar.copy(out=dst, in_=src)
+        wg_bf = [round_wg(a) for a in range(PASSES)]
 
-        w8_bytes = keep.tile([P, N], U8, name="w8_bytes", tag="raw0", align_bytes=64)
+        weights = early.tile([P, M], F32, name="weights", offset=16384, align_bytes=64)
+        nc.sync.dma_start(out=weights[:], in_=wgt)
+        sites = early.tile([P, PACK, M], F32, name="sites", offset=0, align_bytes=64)
+        nc.sync.dma_start(out=sites[:], in_=site.rearrange("(p i) m -> p i m", i=PACK))
+        w8_bytes = early.tile([P, N], U8, name="w8_bytes", offset=20480, align_bytes=64)
         nc.gpsimd.memset(w8_bytes[:].bitcast(I32), 0)
         for q in range(4):
             nc.sync.dma_start(
@@ -136,25 +138,28 @@ def tile_list_syntax_edge_types_kernel(
                 in_=w8_scales[0, 4 * q : 4 * q + 4, :].bitcast(I32),
             )
 
-        wg_codes = [keep.tile([P, H], U32, name="wg_codes%d" % a, align_bytes=64) for a in range(PASSES)]
-        wg_bytes = [keep.tile([P, H], U8, name="wg_bytes%d" % a, align_bytes=64) for a in range(PASSES)]
+        wg_tiles = {}
 
-        def quantize_wg(a):
+        def quantize_wg(a, lo, hi, place):
+            width = (hi - lo) * P
+            if place is None:
+                codes = keep.tile([P, width], U32, name="wg_codes%d_%d" % (a, lo), align_bytes=64)
+            else:
+                codes = relay.tile([P, width], U32, name="wg_codes%d_%d" % (a, lo), offset=place, align_bytes=64)
+            scales = keep.tile([P, width], U8, name="wg_bytes%d_%d" % (a, lo), align_bytes=64)
             nc.vector.quantize_mx(
-                out=wg_codes[a][:].bitcast(FP8X4),
-                scales=wg_bytes[a][:],
-                in_=wg_bf[a][:].rearrange("p i m j -> p (i m j)"),
+                out=codes[:].bitcast(FP8X4),
+                scales=scales[:],
+                in_=wg_bf[a][:, lo:hi].rearrange("p i m j -> p (i m j)"),
             )
+            for i in range(lo, hi):
+                rows = slice((i - lo) * P, (i - lo + 1) * P)
+                wg_tiles[(a, i)] = (codes[:, rows].bitcast(FP8X4), scales[:, rows])
 
-        quantize_wg(0)
-        v1 = [look_up(1, c) for c in range(CHUNKS - 1)]
-
-        dst, src = views(wg_bf[1], 1, 0, P // 2)
-        nc.scalar.copy(out=dst, in_=src)
-        dst, src = views(wg_bf[1], 1, P // 2, P)
-        nc.gpsimd.tensor_scalar(out=dst, in0=src, scalar1=1.0, scalar2=0.0, op0=ALU.mult, op1=ALU.add)
-        quantize_wg(1)
-        v1.append(look_up(1, CHUNKS - 1))
+        quantize_wg(0, 0, PACK, None)
+        quantize_wg(1, 0, 1, None)
+        quantize_wg(1, 1, 3, 0)
+        quantize_wg(1, 3, 4, 4096)
         w8_codes = keep.tile([P, N], I32, name="w8_codes", tag="window1", align_bytes=64)
         nc.sync.dma_start(out=w8_codes[:], in_=w8_words[0].rearrange("p c i -> p (c i)").bitcast(I32))
 
@@ -166,12 +171,12 @@ def tile_list_syntax_edge_types_kernel(
 
         def product(i, c, gate, acc=None, passes=range(PASSES)):
             if acc is None:
-                acc = psum.tile([P, BANK], F32, name="acc", tag="acc")
+                acc = psum.tile([P, BANK], F32, name="acc", tag="gate" if gate else "content")
             rows = slice(i * P, (i + 1) * P)
             for a in passes:
                 codes, scales = table(a, c)
                 if gate:
-                    lhs, lhs_scale = wg_codes[a][:, rows].bitcast(FP8X4), wg_bytes[a][:, rows]
+                    lhs, lhs_scale = wg_tiles[(a, i)]
                 else:
                     lhs, lhs_scale = w4_codes[:, a, rows].bitcast(FP4X4), w4_bytes[:, a, rows]
                 nc.tensor.matmul_mx(
@@ -180,18 +185,17 @@ def tile_list_syntax_edge_types_kernel(
                 )
             return acc
 
-        h = [keep.tile([P, S], F32, name="h%d" % i) for i in range(PACK - 1)]
-        h.append(final.tile([P, S], F32, name="h_last", offset=0, align_bytes=64))
+        h = [keep.tile([P, S], F32, name="h%d" % i) for i in range(PACK)]
 
-        def gated(i, c, content, gate):
-            if i > 0 and c == CHUNKS - 1:
-                sig = relay.tile([P, BANK], F32, name="sig_last%d" % i, offset=(i - 1) * 4096 + 1024)
-            else:
-                sig = ring.tile([P, BANK], F32, name="sig")
-            nc.scalar.activation(out=sig[:], in_=gate[:], func=ACT.Sigmoid)
+        def sigmoid(acc):
+            sig = ring.tile([P, BANK], F32, name="sig", bufs=8)
+            nc.scalar.activation(out=sig[:], in_=acc[:], func=ACT.Sigmoid)
+            return sig
+
+        def gated(i, c, content, sig):
             nc.vector.tensor_tensor(out=h[i][:, c * BANK : (c + 1) * BANK], in0=content[:], in1=sig[:], op=ALU.mult)
 
-        z = [keep.tile([P, 2, SITES, 2], BF16, name="z%d" % u, align_bytes=64) for u in range(EARLY)]
+        z = [keep.tile([P, 2, SITES, 2], BF16, name="z%d" % u, align_bytes=64) for u in range(SITE_CHUNKS)]
 
         def pick(x, i, lo, hi):
             nc.vector.tensor_tensor(
@@ -201,11 +205,6 @@ def tile_list_syntax_edge_types_kernel(
         def add_site(engine, x, i, lo, hi):
             engine.tensor_tensor(out=x, in0=x, in1=sites[:, i, lo:hi], op=ALU.add)
 
-        def squash_after(i, side, x):
-            t = relay.tile([P, BANK], F32, name="t%d_%d" % (i, side), offset=(i - 1) * 4096 + side * 2048)
-            nc.scalar.activation(out=t[:], in_=x, func=ACT.Tanh)
-            return t
-
         def scale(u, i, t):
             dst = z[u][:, i // 2, :, i % 2]
             if i < 2:
@@ -213,15 +212,11 @@ def tile_list_syntax_edge_types_kernel(
             else:
                 nc.vector.tensor_scalar(out=dst, in0=t, scalar1=gains[:, i : i + 1], scalar2=None, op0=ALU.mult)
 
-        def close(u):
-            woven = ring.tile([P, SITES, PACK], BF16, name="woven", bufs=2, align_bytes=64)
-            pairs = z[u][:] if u < EARLY else z_late[:, :, (u - EARLY) * SITES : (u - EARLY + 1) * SITES, :]
+        def scores(u):
+            woven = tail.tile([P, SITES, PACK], BF16, name="woven%d" % u, offset=2048 * u, align_bytes=64)
             nc.vector.tensor_copy(
-                out=woven[:].bitcast(F32), in_=pairs.rearrange("p a m e -> p a (m e)").bitcast(F32).rearrange("p a m -> p m a")
+                out=woven[:].bitcast(F32), in_=z[u][:].rearrange("p a m e -> p a (m e)").bitcast(F32).rearrange("p a m -> p m a")
             )
-            return woven
-
-        def scores(u, woven):
             z_codes = ring.tile([P, SITES], U32, name="z_codes", bufs=2, align_bytes=64)
             z_bytes = ring.tile([P, SITES], U8, name="z_bytes", bufs=2, align_bytes=64)
             nc.vector.quantize_mx(
@@ -229,7 +224,7 @@ def tile_list_syntax_edge_types_kernel(
             )
             banks = []
             for b in range(N // P // PER_BANK):
-                acc = psum.tile([P, PER_BANK, SITES], F32, name="acc2", tag="acc")
+                acc = psum.tile([P, PER_BANK, SITES], F32, name="acc2", tag="gate" if (3 * u + b) % 8 < 4 else "content")
                 for e in range(PER_BANK):
                     types = slice((b * PER_BANK + e) * P, (b * PER_BANK + e + 1) * P)
                     nc.tensor.matmul_mx(
@@ -242,64 +237,57 @@ def tile_list_syntax_edge_types_kernel(
         def store(u, banks):
             for b, acc in enumerate(banks):
                 result = ring.tile([P, PER_BANK, SITES], F32, name="result", bufs=8)
-                if (u, b) in ((3, 0), (3, 2)):
+                if u == SITE_CHUNKS - 1 and b != 1:
                     nc.vector.tensor_copy(out=result[:], in_=acc[:])
                 else:
                     nc.scalar.copy(out=result[:], in_=acc[:])
                 rows = out[b * PER_BANK * P : (b + 1) * PER_BANK * P, u * SITES : (u + 1) * SITES]
                 nc.sync.dma_start(out=rows.rearrange("(e p) m -> p e m", p=P), in_=result[:])
 
-        contents = [product(0, c, False, passes=[0]) for c in range(CHUNKS)]
-        gates = [product(0, c, True, passes=[0]) for c in range(CHUNKS)]
-        for c in range(CHUNKS - 1):
-            product(0, c, False, contents[c], [1])
-        for c in range(CHUNKS):
-            if c == CHUNKS - 1:
-                product(0, c, False, contents[c], [1])
-            gated(0, c, contents[c], product(0, c, True, gates[c], [1]))
         last = PACK - 1
-        late = []
-        for i in range(1, PACK):
-            x = keep.tile([P, M], F32, name="x%d" % (i - 1))
-            pick(x[:], i - 1, 0, M)
-            add_site(nc.gpsimd, x[:], i - 1, 0, M)
+        contents = [product(0, c, False, passes=[0]) for c in range(CHUNKS)]
+        for c in range(CHUNKS):
+            product(0, c, False, contents[c], [1])
+        gates = [product(0, c, True, passes=[0]) for c in range(CHUNKS)]
+        sigs = [sigmoid(product(0, c, True, gates[c], [1])) for c in range(CHUNKS)]
+        xs = []
+        for i in range(PACK):
+            ahead = [sigmoid(product(i + 1, c, True)) for c in range(CHUNKS)] if i < last else []
+            if 1 <= i <= 2:
+                t = relay.tile([P, M], F32, name="t%d" % (i - 1), offset=(i - 1) * 4096, align_bytes=64)
+                nc.scalar.activation(out=t[:], in_=xs[i - 1][:], func=ACT.Tanh)
+                for u in range(SITE_CHUNKS):
+                    scale(u, i - 1, t[:, u * SITES : (u + 1) * SITES])
             for c in range(CHUNKS):
-                content = product(i, c, False)
-                gated(i, c, content, product(i, c, True))
-            early = squash_after(i, 0, x[:, 0:BANK])
-            for u in range(EARLY if i < last else 0):
-                scale(u, i - 1, early[:, u * SITES : (u + 1) * SITES])
-            late.append(squash_after(i, 1, x[:, BANK:M]))
-        z_late = final.tile([P, 2, BANK, 2], BF16, name="z_late", offset=0, align_bytes=64)
+                gated(i, c, contents[c], sigs[c])
+            if i < last:
+                contents = [product(i + 1, c, False) for c in range(CHUNKS)]
+                sigs = ahead
+                x = keep.tile([P, M], F32, name="x%d" % i)
+                pick(x[:], i, 0, M)
+                if i < last - 1:
+                    add_site(nc.gpsimd, x[:], i, 0, M)
+                else:
+                    for half in range(2):
+                        span = slice(half * BANK, (half + 1) * BANK)
+                        add_site(nc.gpsimd, x[:, span], i, half * BANK, (half + 1) * BANK)
+                        nc.scalar.activation(out=x[:, span], in_=x[:, span], func=ACT.Tanh)
+                xs.append(x)
 
-        def scale_late(i, t, lo, hi):
-            nc.vector.tensor_scalar(
-                out=z_late[:, i // 2, lo:hi, i % 2], in0=t, scalar1=gains[:, i : i + 1], scalar2=None, op0=ALU.mult
-            )
-
-        banks = [None] * SITE_CHUNKS
-        picked_last = [None] * SITE_CHUNKS
+        squashed = []
+        banks = []
         for step in range(SITE_CHUNKS + 3):
-            lo, hi = step * SITES, (step + 1) * SITES
             if step < SITE_CHUNKS:
-                x = ring.tile([P, SITES], F32, name="x_last", bufs=2)
+                lo, hi = step * SITES, (step + 1) * SITES
+                place = 2048 * (step - 2) if step >= 2 else 8192 + 1024 * step
+                x = tail.tile([P, SITES], F32, name="x_last%d" % step, offset=place, align_bytes=64)
                 pick(x[:], last, lo, hi)
+                scale(step, last - 1, xs[last - 1][:, lo:hi])
                 add_site(nc.vector, x[:], last, lo, hi)
                 nc.scalar.activation(out=x[:], in_=x[:], func=ACT.Tanh)
-                picked_last[step] = x
-                if step < EARLY:
-                    scale(step, last - 1, early[:, lo:hi])
-                    scale(step, last, x[:])
-            if 1 <= step <= EARLY:
-                banks[step - 1] = scores(step - 1, close(step - 1))
-            if step == SITE_CHUNKS - 1:
-                for i in range(last):
-                    scale_late(i, late[i][:], 0, BANK)
-                for u in range(EARLY, SITE_CHUNKS):
-                    scale_late(last, picked_last[u][:], (u - EARLY) * SITES, (u - EARLY + 1) * SITES)
-            if EARLY <= step - 2 < SITE_CHUNKS:
-                banks[step - 2] = scores(step - 2, close(step - 2))
-            if step in (2, 3):
+                squashed.append(x)
+            if 1 <= step <= SITE_CHUNKS:
+                scale(step - 1, last, squashed[step - 1][:])
+                banks.append(scores(step - 1))
+            if 2 <= step <= SITE_CHUNKS + 1:
                 store(step - 2, banks[step - 2])
-            if step - 3 >= EARLY:
-                store(step - 3, banks[step - 3])

@@ -25,7 +25,7 @@ SITES = 256
 SITE_CHUNKS = M // SITES
 LANES = 16
 PER_BANK = BANK // SITES
-SPLIT = 80
+SPLITS = (80, 44)
 
 
 def tile_list_syntax_edge_types_kernel(
@@ -118,10 +118,14 @@ def tile_list_syntax_edge_types_kernel(
             dst = keep.tile([P, PACK, P, PACK], BF16, name="wg_bf%d" % a, align_bytes=64)
             o = dst[:].rearrange("p i m j -> p m i j")
             s = wg_raw[a][:].rearrange("p j (m i) -> p m i j", i=PACK)
-            nc.scalar.copy(out=o[:, :SPLIT], in_=s[:, :SPLIT])
-            nc.gpsimd.tensor_scalar(
-                out=o[:, SPLIT:], in0=s[:, SPLIT:], scalar1=1.0, scalar2=0.0, op0=ALU.mult, op1=ALU.add
-            )
+            split = SPLITS[a]
+            nc.scalar.copy(out=o[:, :split], in_=s[:, :split])
+            if a == 0:
+                nc.gpsimd.tensor_scalar(
+                    out=o[:, split:], in0=s[:, split:], scalar1=1.0, scalar2=0.0, op0=ALU.mult, op1=ALU.add
+                )
+            else:
+                nc.vector.tensor_copy(out=o[:, split:], in_=s[:, split:])
             return dst
 
         wg_bf = [round_wg(a) for a in range(PASSES)]

@@ -115,17 +115,19 @@ def tile_list_syntax_edge_types_kernel(
         v1 = [look_up(c) for c in range(CHUNKS)]
 
         def round_wg(a):
-            dst = keep.tile([P, PACK, P, PACK], BF16, name="wg_bf%d" % a, align_bytes=64)
+            dst = keep.tile([P, PACK, P, PACK], BF16, name="wg_bf%d" % a, tag="wg_bf%d" % a, align_bytes=64)
             o = dst[:].rearrange("p i m j -> p m i j")
             s = wg_raw[a][:].rearrange("p j (m i) -> p m i j", i=PACK)
             split = SPLITS[a]
-            nc.scalar.copy(out=o[:, :split], in_=s[:, :split])
+            o_run = dst[:].rearrange("p i m j -> p m j i")
+            s_run = wg_raw[a][:].rearrange("p j (m i) -> p m j i", i=PACK)
+            nc.scalar.copy(out=o_run[:, :split], in_=s_run[:, :split])
             if a == 0:
                 nc.gpsimd.tensor_scalar(
                     out=o[:, split:], in0=s[:, split:], scalar1=1.0, scalar2=0.0, op0=ALU.mult, op1=ALU.add
                 )
             else:
-                nc.vector.tensor_copy(out=o[:, split:], in_=s[:, split:])
+                nc.vector.tensor_copy(out=o_run[:, split:], in_=s_run[:, split:])
             return dst
 
         wg_bf = [round_wg(a) for a in range(PASSES)]
@@ -134,14 +136,6 @@ def tile_list_syntax_edge_types_kernel(
         nc.sync.dma_start(out=weights[:], in_=wgt)
         sites = early.tile([P, PACK, M], F32, name="sites", offset=0, align_bytes=64)
         nc.sync.dma_start(out=sites[:], in_=site.rearrange("(p i) m -> p i m", i=PACK))
-        w8_bytes = early.tile([P, N], U8, name="w8_bytes", offset=20480, align_bytes=64)
-        nc.gpsimd.memset(w8_bytes[:].bitcast(I32), 0)
-        for q in range(4):
-            nc.sync.dma_start(
-                out=w8_bytes[32 * q : 32 * q + 4, :].bitcast(I32),
-                in_=w8_scales[0, 4 * q : 4 * q + 4, :].bitcast(I32),
-            )
-
         wg_tiles = {}
 
         def quantize_wg(a, lo, hi, place):
@@ -164,6 +158,14 @@ def tile_list_syntax_edge_types_kernel(
         quantize_wg(1, 0, 1, None)
         quantize_wg(1, 1, 3, 0)
         quantize_wg(1, 3, 4, 4096)
+        w8_bytes = keep.tile([P, N], U8, name="w8_bytes", tag="wg_bf1", align_bytes=64)
+        nc.gpsimd.memset(w8_bytes[:].bitcast(I32), 0)
+        for q in range(4):
+            nc.sync.dma_start(
+                out=w8_bytes[32 * q : 32 * q + 4, :].bitcast(I32),
+                in_=w8_scales[0, 4 * q : 4 * q + 4, :].bitcast(I32),
+            )
+
         w8_codes = keep.tile([P, N], I32, name="w8_codes", tag="window1", align_bytes=64)
         nc.sync.dma_start(out=w8_codes[:], in_=w8_words[0].rearrange("p c i -> p (c i)").bitcast(I32))
 

@@ -140,10 +140,8 @@ def tile_list_syntax_edge_types_kernel(
 
         def quantize_wg(a, lo, hi, place):
             width = (hi - lo) * P
-            if place is None:
-                codes = keep.tile([P, width], U32, name="wg_codes%d_%d" % (a, lo), align_bytes=64)
-            else:
-                codes = relay.tile([P, width], U32, name="wg_codes%d_%d" % (a, lo), offset=place, align_bytes=64)
+            pool, offset = place
+            codes = pool.tile([P, width], U32, name="wg_codes%d_%d" % (a, lo), offset=offset, align_bytes=64)
             scales = keep.tile([P, width], U8, name="wg_bytes%d_%d" % (a, lo), align_bytes=64)
             nc.vector.quantize_mx(
                 out=codes[:].bitcast(FP8X4),
@@ -154,10 +152,12 @@ def tile_list_syntax_edge_types_kernel(
                 rows = slice((i - lo) * P, (i - lo + 1) * P)
                 wg_tiles[(a, i)] = (codes[:, rows].bitcast(FP8X4), scales[:, rows])
 
-        quantize_wg(0, 0, PACK, None)
-        quantize_wg(1, 0, 1, None)
-        quantize_wg(1, 1, 3, 0)
-        quantize_wg(1, 3, 4, 4096)
+        quantize_wg(0, 0, 1, (early, 28672))
+        quantize_wg(1, 0, 1, (early, 29184))
+        quantize_wg(0, 1, 2, (early, 20480))
+        quantize_wg(1, 1, 3, (relay, 0))
+        quantize_wg(0, 2, 4, (early, 20992))
+        quantize_wg(1, 3, 4, (relay, 4096))
         w8_bytes = keep.tile([P, N], U8, name="w8_bytes", tag="wg_bf1", align_bytes=64)
         nc.gpsimd.memset(w8_bytes[:].bitcast(I32), 0)
         for q in range(4):

@@ -25,7 +25,7 @@ SITES = 256
 SITE_CHUNKS = M // SITES
 LANES = 16
 PER_BANK = BANK // SITES
-SPLITS = (80, 44)
+SPLITS = (80, 34)
 
 
 def tile_list_syntax_edge_types_kernel(

@@ -26,6 +26,7 @@ SITE_CHUNKS = M // SITES
 LANES = 16
 PER_BANK = BANK // SITES
 SPLITS = (80, 34)
+POOL_SITES = 768
 
 
 def tile_list_syntax_edge_types_kernel(
@@ -39,6 +40,7 @@ def tile_list_syntax_edge_types_kernel(
         early = ctx.enter_context(tc.tile_pool(name="early", bufs=1))
         tail = ctx.enter_context(tc.tile_pool(name="tail", bufs=1))
         relay = ctx.enter_context(tc.tile_pool(name="relay", bufs=1))
+        dealt = ctx.enter_context(tc.tile_pool(name="dealt", bufs=1))
         ring = ctx.enter_context(tc.tile_pool(name="ring", bufs=4))
         psum = ctx.enter_context(tc.psum_pool(name="psum", bufs=4))
 
@@ -85,11 +87,11 @@ def tile_list_syntax_edge_types_kernel(
                 )
 
         move_scales(0)
-        w4_codes = keep.tile([P, PASSES, H], U16, name="w4_codes", align_bytes=64)
-        nc.vector.tensor_copy(
-            out=w4_codes[:].rearrange("p a (i m) -> p a i m", i=PACK),
-            in_=w4_raw[:].rearrange("p a (m i) -> p a i m", i=PACK),
-        )
+        w4_codes = []
+        for i in range(PACK):
+            codes = dealt.tile([P, PASSES, P], U16, name="w4_codes%d" % i, offset=1024 * i, align_bytes=64)
+            nc.vector.tensor_copy(out=codes[:], in_=w4_raw[:].rearrange("p a (m i) -> p a i m", i=PACK)[:, :, i, :])
+            w4_codes.append(codes)
         wg_raw = [early.tile([P, PACK, H], F32, name="wg_raw%d" % a, offset=12288 + 8192 * a, align_bytes=64) for a in range(PASSES)]
         for a in range(PASSES):
             nc.sync.dma_start(
@@ -184,7 +186,7 @@ def tile_list_syntax_edge_types_kernel(
                 if gate:
                     lhs, lhs_scale = wg_tiles[(a, i)]
                 else:
-                    lhs, lhs_scale = w4_codes[:, a, rows].bitcast(FP4X4), w4_bytes[:, a, rows]
+                    lhs, lhs_scale = w4_codes[i][:, a, :].bitcast(FP4X4), w4_bytes[:, a, rows]
                 nc.tensor.matmul_mx(
                     out=acc[:], lhsT=lhs, lhsT_scale=lhs_scale, rhs=codes, rhs_scale=scales,
                     start=(a == 0), stop=(a == PASSES - 1),
@@ -208,8 +210,8 @@ def tile_list_syntax_edge_types_kernel(
                 out=x, in0=h[i][:].indirect(idx2[:, lo // LANES : hi // LANES]), in1=weights[:, lo:hi], op=ALU.mult
             )
 
-        def add_site(engine, x, i, lo, hi):
-            engine.tensor_tensor(out=x, in0=x, in1=sites[:, i, lo:hi], op=ALU.add)
+        def add_site(engine, y, x, i, lo, hi):
+            engine.tensor_tensor(out=y, in0=x, in1=sites[:, i, lo:hi], op=ALU.add)
 
         def scale(u, i, t):
             dst = z[u][:, i // 2, :, i % 2]
@@ -259,25 +261,26 @@ def tile_list_syntax_edge_types_kernel(
         xs = []
         for i in range(PACK):
             ahead = [sigmoid(product(i + 1, c, True)) for c in range(CHUNKS)] if i < last else []
-            if 1 <= i <= 2:
-                t = relay.tile([P, M], F32, name="t%d" % (i - 1), offset=(i - 1) * 4096, align_bytes=64)
-                nc.scalar.activation(out=t[:], in_=xs[i - 1][:], func=ACT.Tanh)
-                for u in range(SITE_CHUNKS):
-                    scale(u, i - 1, t[:, u * SITES : (u + 1) * SITES])
             for c in range(CHUNKS):
                 gated(i, c, contents[c], sigs[c])
+            if i >= 1:
+                rest = dealt.tile([P, M - POOL_SITES], F32, name="rest%d" % (i - 1), offset=1024 * i, align_bytes=64)
+                add_site(nc.vector, rest[:], xs[i - 1][:, POOL_SITES:], i - 1, POOL_SITES, M)
+                if i < last:
+                    t = relay.tile([P, M], F32, name="t%d" % (i - 1), offset=(i - 1) * 4096, align_bytes=64)
+                else:
+                    t = xs[i - 1]
+                nc.scalar.activation(out=t[:, :POOL_SITES], in_=xs[i - 1][:, :POOL_SITES], func=ACT.Tanh)
+                nc.scalar.activation(out=t[:, POOL_SITES:], in_=rest[:], func=ACT.Tanh)
+                if i < last:
+                    for u in range(SITE_CHUNKS):
+                        scale(u, i - 1, t[:, u * SITES : (u + 1) * SITES])
             if i < last:
                 contents = [product(i + 1, c, False) for c in range(CHUNKS)]
                 sigs = ahead
                 x = keep.tile([P, M], F32, name="x%d" % i)
                 pick(x[:], i, 0, M)
-                if i < last - 1:
-                    add_site(nc.gpsimd, x[:], i, 0, M)
-                else:
-                    for half in range(2):
-                        span = slice(half * BANK, (half + 1) * BANK)
-                        add_site(nc.gpsimd, x[:, span], i, half * BANK, (half + 1) * BANK)
-                        nc.scalar.activation(out=x[:, span], in_=x[:, span], func=ACT.Tanh)
+                add_site(nc.gpsimd, x[:, :POOL_SITES], x[:, :POOL_SITES], i, 0, POOL_SITES)
                 xs.append(x)
 
         squashed = []
@@ -289,7 +292,7 @@ def tile_list_syntax_edge_types_kernel(
                 x = tail.tile([P, SITES], F32, name="x_last%d" % step, offset=place, align_bytes=64)
                 pick(x[:], last, lo, hi)
                 scale(step, last - 1, xs[last - 1][:, lo:hi])
-                add_site(nc.vector, x[:], last, lo, hi)
+                add_site(nc.vector, x[:], x[:], last, lo, hi)
                 nc.scalar.activation(out=x[:], in_=x[:], func=ACT.Tanh)
                 squashed.append(x)
             if 1 <= step <= SITE_CHUNKS:

@@ -263,23 +263,22 @@ def tile_list_syntax_edge_types_kernel(
             ahead = [sigmoid(product(i + 1, c, True)) for c in range(CHUNKS)] if i < last else []
             for c in range(CHUNKS):
                 gated(i, c, contents[c], sigs[c])
-            if i >= 1:
+            if 1 <= i < last:
                 rest = dealt.tile([P, M - POOL_SITES], F32, name="rest%d" % (i - 1), offset=1024 * i, align_bytes=64)
                 add_site(nc.vector, rest[:], xs[i - 1][:, POOL_SITES:], i - 1, POOL_SITES, M)
-                if i < last:
-                    t = relay.tile([P, M], F32, name="t%d" % (i - 1), offset=(i - 1) * 4096, align_bytes=64)
-                else:
-                    t = xs[i - 1]
+                t = relay.tile([P, M], F32, name="t%d" % (i - 1), offset=(i - 1) * 4096, align_bytes=64)
                 nc.scalar.activation(out=t[:, :POOL_SITES], in_=xs[i - 1][:, :POOL_SITES], func=ACT.Tanh)
                 nc.scalar.activation(out=t[:, POOL_SITES:], in_=rest[:], func=ACT.Tanh)
-                if i < last:
-                    for u in range(SITE_CHUNKS):
-                        scale(u, i - 1, t[:, u * SITES : (u + 1) * SITES])
+                for u in range(SITE_CHUNKS):
+                    scale(u, i - 1, t[:, u * SITES : (u + 1) * SITES])
+            if i == last:
+                nc.scalar.activation(out=xs[i - 1][:], in_=xs[i - 1][:], func=ACT.Tanh)
             if i < last:
                 contents = [product(i + 1, c, False) for c in range(CHUNKS)]
                 sigs = ahead
-                x = keep.tile([P, M], F32, name="x%d" % i)
-                pick(x[:], i, 0, M)
+                width = M if i < last - 1 else POOL_SITES
+                x = keep.tile([P, width], F32, name="x%d" % i)
+                pick(x[:], i, 0, width)
                 add_site(nc.gpsimd, x[:, :POOL_SITES], x[:, :POOL_SITES], i, 0, POOL_SITES)
                 xs.append(x)
 
@@ -291,10 +290,15 @@ def tile_list_syntax_edge_types_kernel(
                 place = 2048 * (step - 2) if step >= 2 else 8192 + 1024 * step
                 x = tail.tile([P, SITES], F32, name="x_last%d" % step, offset=place, align_bytes=64)
                 pick(x[:], last, lo, hi)
-                scale(step, last - 1, xs[last - 1][:, lo:hi])
+                scale(step, last - 1, xs[last - 1][:, lo:hi] if hi <= POOL_SITES else rest[:])
                 add_site(nc.vector, x[:], x[:], last, lo, hi)
                 nc.scalar.activation(out=x[:], in_=x[:], func=ACT.Tanh)
                 squashed.append(x)
+            if step == 1:
+                rest = dealt.tile([P, M - POOL_SITES], F32, name="rest2", offset=1024 * last, align_bytes=64)
+                pick(rest[:], last - 1, POOL_SITES, M)
+                add_site(nc.vector, rest[:], rest[:], last - 1, POOL_SITES, M)
+                nc.scalar.activation(out=rest[:], in_=rest[:], func=ACT.Tanh)
             if 1 <= step <= SITE_CHUNKS:
                 scale(step - 1, last, squashed[step - 1][:])
                 banks.append(scores(step - 1))

@@ -27,6 +27,7 @@ LANES = 16
 PER_BANK = BANK // SITES
 SPLITS = (80, 34)
 POOL_SITES = 768
+ALIGN = 256
 
 
 def tile_list_syntax_edge_types_kernel(
@@ -44,9 +45,9 @@ def tile_list_syntax_edge_types_kernel(
         ring = ctx.enter_context(tc.tile_pool(name="ring", bufs=4))
         psum = ctx.enter_context(tc.psum_pool(name="psum", bufs=4))
 
-        w4_bytes_raw = keep.tile([P, PASSES, H], U8, name="w4_bytes_raw", align_bytes=64)
+        w4_bytes_raw = keep.tile([P, PASSES, H], U8, name="w4_bytes_raw", align_bytes=ALIGN)
         nc.gpsimd.memset(w4_bytes_raw[:].rearrange("p a c -> p (a c)").bitcast(I32), 0)
-        tab_bytes = keep.tile([P, T], U8, name="tab_bytes", align_bytes=64)
+        tab_bytes = keep.tile([P, T], U8, name="tab_bytes", align_bytes=ALIGN)
         nc.sync.dma_start(
             out=tab_bytes[0:32, :].bitcast(I32), in_=tab_scales.rearrange("a q t -> (a q) t").bitcast(I32)
         )
@@ -59,24 +60,24 @@ def tile_list_syntax_edge_types_kernel(
                 out=w4_bytes_raw[32 * q : 32 * q + 4, :, :].bitcast(I32),
                 in_=w4_scales[:, 4 * q : 4 * q + 4, :].rearrange("a r c -> r a c").bitcast(I32),
             )
-        w4_raw = early.tile([P, PASSES, H], U16, name="w4_raw", offset=19456, align_bytes=64)
+        w4_raw = early.tile([P, PASSES, H], U16, name="w4_raw", offset=19456, align_bytes=ALIGN)
         nc.sync.dma_start(out=w4_raw[:].bitcast(I32), in_=w4_words.rearrange("a p c -> p a c").bitcast(I32))
         tab = [
-            shared.tile([P, T], I32, name="tab0", offset=0, align_bytes=64),
-            keep.tile([P, T], I32, name="tab1", tag="window1", align_bytes=64),
+            shared.tile([P, T], I32, name="tab0", offset=0, align_bytes=ALIGN),
+            keep.tile([P, T], I32, name="tab1", tag="window1", align_bytes=ALIGN),
         ]
         for a in range(PASSES):
             nc.sync.dma_start(out=tab[a][:], in_=tab_words[a].rearrange("p t i -> p (t i)").bitcast(I32))
         idx2 = lists.tile([P, M // LANES], U16, name="idx2")
         nc.sync.dma_start(idx2[:], offs2)
-        v_bytes = [keep.tile([P, S], U8, name="v_bytes%d" % a, align_bytes=64) for a in range(PASSES)]
+        v_bytes = [keep.tile([P, S], U8, name="v_bytes%d" % a, align_bytes=ALIGN) for a in range(PASSES)]
         nc.vector.memset(v_bytes[0][:].bitcast(I32), 0)
         nc.gpsimd.memset(v_bytes[1][:].bitcast(I32), 0)
 
         gains = keep.tile([P, PACK], F32, name="gains")
         nc.gpsimd.dma_start(out=gains[:], in_=gain.rearrange("(p i) -> p i", i=PACK))
 
-        picked = keep.tile([P, S], U8, name="picked", align_bytes=64)
+        picked = keep.tile([P, S], U8, name="picked", align_bytes=ALIGN)
         nc.vector.tensor_copy(out=picked[:], in_=tab_bytes[:].indirect(idx[:]))
 
         def move_scales(a):
@@ -89,10 +90,10 @@ def tile_list_syntax_edge_types_kernel(
         move_scales(0)
         w4_codes = []
         for i in range(PACK):
-            codes = dealt.tile([P, PASSES, P], U16, name="w4_codes%d" % i, offset=1024 * i, align_bytes=64)
+            codes = dealt.tile([P, PASSES, P], U16, name="w4_codes%d" % i, offset=1024 * i, align_bytes=ALIGN)
             nc.vector.tensor_copy(out=codes[:], in_=w4_raw[:].rearrange("p a (m i) -> p a i m", i=PACK)[:, :, i, :])
             w4_codes.append(codes)
-        wg_raw = [early.tile([P, PACK, H], F32, name="wg_raw%d" % a, offset=12288 + 8192 * a, align_bytes=64) for a in range(PASSES)]
+        wg_raw = [early.tile([P, PACK, H], F32, name="wg_raw%d" % a, offset=12288 + 8192 * a, align_bytes=ALIGN) for a in range(PASSES)]
         for a in range(PASSES):
             nc.sync.dma_start(
                 out=wg_raw[a][:], in_=wg[a * P * PACK : (a + 1) * P * PACK, :].rearrange("(p j) c -> p j c", j=PACK)
@@ -103,13 +104,13 @@ def tile_list_syntax_edge_types_kernel(
         cols = BANK // LANES
 
         def look_up(c):
-            piece = keep.tile([P, BANK], U32, name="v1_%d" % c, tag="v1_%d" % c, align_bytes=64)
+            piece = keep.tile([P, BANK], U32, name="v1_%d" % c, tag="v1_%d" % c, align_bytes=ALIGN)
             nc.vector.tensor_copy(out=piece[:], in_=tab[1][:].bitcast(U32).indirect(idx[:, c * cols : (c + 1) * cols]))
             return piece
 
-        v0 = keep.tile([P, S], U32, name="v0", align_bytes=64)
+        v0 = keep.tile([P, S], U32, name="v0", align_bytes=ALIGN)
         nc.vector.tensor_copy(out=v0[:], in_=tab[0][:].bitcast(U32).indirect(idx[:]))
-        w4_bytes = keep.tile([P, PASSES, H], U8, name="w4_bytes", align_bytes=64)
+        w4_bytes = keep.tile([P, PASSES, H], U8, name="w4_bytes", align_bytes=ALIGN)
         nc.vector.tensor_copy(
             out=w4_bytes[:].rearrange("p a (i m) -> p a i m", i=PACK),
             in_=w4_bytes_raw[:].rearrange("p a (m i) -> p a i m", i=PACK),
@@ -117,7 +118,7 @@ def tile_list_syntax_edge_types_kernel(
         v1 = [look_up(c) for c in range(CHUNKS)]
 
         def round_wg(a):
-            dst = keep.tile([P, PACK, P, PACK], BF16, name="wg_bf%d" % a, tag="wg_bf%d" % a, align_bytes=64)
+            dst = keep.tile([P, PACK, P, PACK], BF16, name="wg_bf%d" % a, tag="wg_bf%d" % a, align_bytes=ALIGN)
             o = dst[:].rearrange("p i m j -> p m i j")
             s = wg_raw[a][:].rearrange("p j (m i) -> p m i j", i=PACK)
             split = SPLITS[a]
@@ -134,17 +135,17 @@ def tile_list_syntax_edge_types_kernel(
 
         wg_bf = [round_wg(a) for a in range(PASSES)]
 
-        weights = early.tile([P, M], F32, name="weights", offset=16384, align_bytes=64)
+        weights = early.tile([P, M], F32, name="weights", offset=16384, align_bytes=ALIGN)
         nc.sync.dma_start(out=weights[:], in_=wgt)
-        sites = early.tile([P, PACK, M], F32, name="sites", offset=0, align_bytes=64)
+        sites = early.tile([P, PACK, M], F32, name="sites", offset=0, align_bytes=ALIGN)
         nc.sync.dma_start(out=sites[:], in_=site.rearrange("(p i) m -> p i m", i=PACK))
         wg_tiles = {}
 
         def quantize_wg(a, lo, hi, place):
             width = (hi - lo) * P
             pool, offset = place
-            codes = pool.tile([P, width], U32, name="wg_codes%d_%d" % (a, lo), offset=offset, align_bytes=64)
-            scales = keep.tile([P, width], U8, name="wg_bytes%d_%d" % (a, lo), align_bytes=64)
+            codes = pool.tile([P, width], U32, name="wg_codes%d_%d" % (a, lo), offset=offset, align_bytes=ALIGN)
+            scales = keep.tile([P, width], U8, name="wg_bytes%d_%d" % (a, lo), align_bytes=ALIGN)
             nc.vector.quantize_mx(
                 out=codes[:].bitcast(FP8X4),
                 scales=scales[:],
@@ -160,7 +161,7 @@ def tile_list_syntax_edge_types_kernel(
         quantize_wg(1, 1, 3, (relay, 0))
         quantize_wg(0, 2, 4, (early, 20992))
         quantize_wg(1, 3, 4, (relay, 4096))
-        w8_bytes = keep.tile([P, N], U8, name="w8_bytes", tag="wg_bf1", align_bytes=64)
+        w8_bytes = keep.tile([P, N], U8, name="w8_bytes", tag="wg_bf1", align_bytes=ALIGN)
         nc.gpsimd.memset(w8_bytes[:].bitcast(I32), 0)
         for q in range(4):
             nc.sync.dma_start(
@@ -168,7 +169,7 @@ def tile_list_syntax_edge_types_kernel(
                 in_=w8_scales[0, 4 * q : 4 * q + 4, :].bitcast(I32),
             )
 
-        w8_codes = keep.tile([P, N], I32, name="w8_codes", tag="window1", align_bytes=64)
+        w8_codes = keep.tile([P, N], I32, name="w8_codes", tag="window1", align_bytes=ALIGN)
         nc.sync.dma_start(out=w8_codes[:], in_=w8_words[0].rearrange("p c i -> p (c i)").bitcast(I32))
 
         def table(a, c):
@@ -193,17 +194,17 @@ def tile_list_syntax_edge_types_kernel(
                 )
             return acc
 
-        h = [keep.tile([P, S], F32, name="h%d" % i) for i in range(PACK)]
+        h = [keep.tile([P, S], F32, name="h%d" % i, align_bytes=ALIGN) for i in range(PACK)]
 
         def sigmoid(acc):
-            sig = ring.tile([P, BANK], F32, name="sig", bufs=8)
+            sig = ring.tile([P, BANK], F32, name="sig", bufs=8, align_bytes=ALIGN)
             nc.scalar.activation(out=sig[:], in_=acc[:], func=ACT.Sigmoid)
             return sig
 
         def gated(i, c, content, sig):
             nc.vector.tensor_tensor(out=h[i][:, c * BANK : (c + 1) * BANK], in0=content[:], in1=sig[:], op=ALU.mult)
 
-        z = [keep.tile([P, 2, SITES, 2], BF16, name="z%d" % u, align_bytes=64) for u in range(SITE_CHUNKS)]
+        z = [keep.tile([P, 2, SITES, 2], BF16, name="z%d" % u, align_bytes=ALIGN) for u in range(SITE_CHUNKS)]
 
         def pick(x, i, lo, hi):
             nc.vector.tensor_tensor(
@@ -221,12 +222,12 @@ def tile_list_syntax_edge_types_kernel(
                 nc.vector.tensor_scalar(out=dst, in0=t, scalar1=gains[:, i : i + 1], scalar2=None, op0=ALU.mult)
 
         def scores(u):
-            woven = tail.tile([P, SITES, PACK], BF16, name="woven%d" % u, offset=2048 * u, align_bytes=64)
+            woven = tail.tile([P, SITES, PACK], BF16, name="woven%d" % u, offset=2048 * u, align_bytes=ALIGN)
             nc.vector.tensor_copy(
                 out=woven[:].bitcast(F32), in_=z[u][:].rearrange("p a m e -> p a (m e)").bitcast(F32).rearrange("p a m -> p m a")
             )
-            z_codes = ring.tile([P, SITES], U32, name="z_codes", bufs=2, align_bytes=64)
-            z_bytes = ring.tile([P, SITES], U8, name="z_bytes", bufs=2, align_bytes=64)
+            z_codes = ring.tile([P, SITES], U32, name="z_codes", bufs=2, align_bytes=ALIGN)
+            z_bytes = ring.tile([P, SITES], U8, name="z_bytes", bufs=2, align_bytes=ALIGN)
             nc.vector.quantize_mx(
                 out=z_codes[:].bitcast(FP8X4), scales=z_bytes[:], in_=woven[:].rearrange("p m i -> p (m i)")
             )
@@ -244,7 +245,7 @@ def tile_list_syntax_edge_types_kernel(
 
         def store(u, banks):
             for b, acc in enumerate(banks):
-                result = ring.tile([P, PER_BANK, SITES], F32, name="result", bufs=8)
+                result = ring.tile([P, PER_BANK, SITES], F32, name="result", bufs=8, align_bytes=ALIGN)
                 if u == SITE_CHUNKS - 1 and b != 1:
                     nc.vector.tensor_copy(out=result[:], in_=acc[:])
                 else:
@@ -264,9 +265,9 @@ def tile_list_syntax_edge_types_kernel(
             for c in range(CHUNKS):
                 gated(i, c, contents[c], sigs[c])
             if 1 <= i < last:
-                rest = dealt.tile([P, M - POOL_SITES], F32, name="rest%d" % (i - 1), offset=1024 * i, align_bytes=64)
+                rest = dealt.tile([P, M - POOL_SITES], F32, name="rest%d" % (i - 1), offset=1024 * i, align_bytes=ALIGN)
                 add_site(nc.vector, rest[:], xs[i - 1][:, POOL_SITES:], i - 1, POOL_SITES, M)
-                t = relay.tile([P, M], F32, name="t%d" % (i - 1), offset=(i - 1) * 4096, align_bytes=64)
+                t = relay.tile([P, M], F32, name="t%d" % (i - 1), offset=(i - 1) * 4096, align_bytes=ALIGN)
                 nc.scalar.activation(out=t[:, :POOL_SITES], in_=xs[i - 1][:, :POOL_SITES], func=ACT.Tanh)
                 nc.scalar.activation(out=t[:, POOL_SITES:], in_=rest[:], func=ACT.Tanh)
                 for u in range(SITE_CHUNKS):
@@ -277,7 +278,7 @@ def tile_list_syntax_edge_types_kernel(
                 contents = [product(i + 1, c, False) for c in range(CHUNKS)]
                 sigs = ahead
                 width = M if i < last - 1 else POOL_SITES
-                x = keep.tile([P, width], F32, name="x%d" % i)
+                x = keep.tile([P, width], F32, name="x%d" % i, align_bytes=ALIGN)
                 pick(x[:], i, 0, width)
                 add_site(nc.gpsimd, x[:, :POOL_SITES], x[:, :POOL_SITES], i, 0, POOL_SITES)
                 xs.append(x)
@@ -288,14 +289,14 @@ def tile_list_syntax_edge_types_kernel(
             if step < SITE_CHUNKS:
                 lo, hi = step * SITES, (step + 1) * SITES
                 place = 2048 * (step - 2) if step >= 2 else 8192 + 1024 * step
-                x = tail.tile([P, SITES], F32, name="x_last%d" % step, offset=place, align_bytes=64)
+                x = tail.tile([P, SITES], F32, name="x_last%d" % step, offset=place, align_bytes=ALIGN)
                 pick(x[:], last, lo, hi)
                 scale(step, last - 1, xs[last - 1][:, lo:hi] if hi <= POOL_SITES else rest[:])
                 add_site(nc.vector, x[:], x[:], last, lo, hi)
                 nc.scalar.activation(out=x[:], in_=x[:], func=ACT.Tanh)
                 squashed.append(x)
             if step == 1:
-                rest = dealt.tile([P, M - POOL_SITES], F32, name="rest2", offset=1024 * last, align_bytes=64)
+                rest = dealt.tile([P, M - POOL_SITES], F32, name="rest2", offset=1024 * last, align_bytes=ALIGN)
                 pick(rest[:], last - 1, POOL_SITES, M)
                 add_site(nc.vector, rest[:], rest[:], last - 1, POOL_SITES, M)
                 nc.scalar.activation(out=rest[:], in_=rest[:], func=ACT.Tanh)

@@ -43,6 +43,7 @@ def tile_list_syntax_edge_types_kernel(
         relay = ctx.enter_context(tc.tile_pool(name="relay", bufs=1))
         dealt = ctx.enter_context(tc.tile_pool(name="dealt", bufs=1))
         ring = ctx.enter_context(tc.tile_pool(name="ring", bufs=4))
+        spare = ctx.enter_context(tc.tile_pool(name="spare", bufs=1))
         psum = ctx.enter_context(tc.psum_pool(name="psum", bufs=4))
 
         w4_bytes_raw = keep.tile([P, PASSES, H], U8, name="w4_bytes_raw", align_bytes=ALIGN)
@@ -55,10 +56,10 @@ def tile_list_syntax_edge_types_kernel(
         nc.vector.memset(tab_bytes[64:128, :].bitcast(I32), 0)
         idx = lists.tile([P, S // LANES], U16, name="idx")
         nc.sync.dma_start(idx[:], offs)
-        for q in range(4):
+        for r in range(4):
             nc.sync.dma_start(
-                out=w4_bytes_raw[32 * q : 32 * q + 4, :, :].bitcast(I32),
-                in_=w4_scales[:, 4 * q : 4 * q + 4, :].rearrange("a r c -> r a c").bitcast(I32),
+                out=w4_bytes_raw[r:P:32, :, :].bitcast(I32),
+                in_=w4_scales[:, r:16:4, :].rearrange("a q c -> q a c").bitcast(I32),
             )
         w4_raw = early.tile([P, PASSES, H], U16, name="w4_raw", offset=19456, align_bytes=ALIGN)
         nc.sync.dma_start(out=w4_raw[:].bitcast(I32), in_=w4_words.rearrange("a p c -> p a c").bitcast(I32))
@@ -81,10 +82,10 @@ def tile_list_syntax_edge_types_kernel(
         nc.vector.tensor_copy(out=picked[:], in_=tab_bytes[:].indirect(idx[:]))
 
         def move_scales(a):
-            for q in range(4):
+            for r in range(4):
                 nc.sync.dma_start(
-                    out=v_bytes[a][32 * q : 32 * q + 4, :].bitcast(I32),
-                    in_=picked[16 * a + 4 * q : 16 * a + 4 * q + 4, :].bitcast(I32),
+                    out=v_bytes[a][r:P:32, :].bitcast(I32),
+                    in_=picked[16 * a + r : 16 * a + 16 : 4, :].bitcast(I32),
                 )
 
         move_scales(0)
@@ -133,6 +134,8 @@ def tile_list_syntax_edge_types_kernel(
                 nc.vector.tensor_copy(out=o_run[:, split:], in_=s_run[:, split:])
             return dst
 
+        warm = spare.tile([P, 1], F32, name="warm")
+        nc.scalar.activation(out=warm[:], in_=wg_raw[0][:, 0, 0:1], func=ACT.Sigmoid)
         wg_bf = [round_wg(a) for a in range(PASSES)]
 
         weights = early.tile([P, M], F32, name="weights", offset=16384, align_bytes=ALIGN)
@@ -178,7 +181,7 @@ def tile_list_syntax_edge_types_kernel(
                 return v0[:, span].bitcast(FP8X4), v_bytes[0][:, span]
             return v1[c][:].bitcast(FP8X4), v_bytes[1][:, span]
 
-        def product(i, c, gate, acc=None, passes=range(PASSES)):
+        def product(i, c, gate, acc=None, passes=range(PASSES), first=0):
             if acc is None:
                 acc = psum.tile([P, BANK], F32, name="acc", tag="gate" if gate else "content")
             rows = slice(i * P, (i + 1) * P)
@@ -190,7 +193,7 @@ def tile_list_syntax_edge_types_kernel(
                     lhs, lhs_scale = w4_codes[i][:, a, :].bitcast(FP4X4), w4_bytes[:, a, rows]
                 nc.tensor.matmul_mx(
                     out=acc[:], lhsT=lhs, lhsT_scale=lhs_scale, rhs=codes, rhs_scale=scales,
-                    start=(a == 0), stop=(a == PASSES - 1),
+                    start=(a == first), stop=(a != first),
                 )
             return acc
 
@@ -254,11 +257,16 @@ def tile_list_syntax_edge_types_kernel(
                 nc.sync.dma_start(out=rows.rearrange("(e p) m -> p e m", p=P), in_=result[:])
 
         last = PACK - 1
-        contents = [product(0, c, False, passes=[0]) for c in range(CHUNKS)]
+        half = CHUNKS // 2
+        contents = [None if c == half else product(0, c, False, passes=[0]) for c in range(CHUNKS)]
         for c in range(CHUNKS):
-            product(0, c, False, contents[c], [1])
-        gates = [product(0, c, True, passes=[0]) for c in range(CHUNKS)]
-        sigs = [sigmoid(product(0, c, True, gates[c], [1])) for c in range(CHUNKS)]
+            if c == half:
+                contents[c] = product(0, c, False, passes=[1, 0], first=1)
+            else:
+                product(0, c, False, contents[c], [1])
+        gates = [product(0, c, True, passes=[0]) for c in range(half)]
+        sigs = [sigmoid(product(0, c, True, gates[c], [1])) for c in range(half)]
+        sigs.extend(sigmoid(product(0, c, True, passes=[1, 0], first=1)) for c in range(half, CHUNKS))
         xs = []
         for i in range(PACK):
             ahead = [sigmoid(product(i + 1, c, True)) for c in range(CHUNKS)] if i < last else []

@@ -25,7 +25,7 @@ SITES = 256
 SITE_CHUNKS = M // SITES
 LANES = 16
 PER_BANK = BANK // SITES
-SPLITS = (80, 34)
+SPLITS = (72, 46)
 POOL_SITES = 768
 ALIGN = 256
 
@@ -46,7 +46,7 @@ def tile_list_syntax_edge_types_kernel(
         spare = ctx.enter_context(tc.tile_pool(name="spare", bufs=1))
         psum = ctx.enter_context(tc.psum_pool(name="psum", bufs=4))
 
-        w4_bytes_raw = keep.tile([P, PASSES, H], U8, name="w4_bytes_raw", align_bytes=ALIGN)
+        w4_bytes_raw = early.tile([P, PASSES, H], U8, name="w4_bytes_raw", offset=19968, align_bytes=ALIGN)
         nc.gpsimd.memset(w4_bytes_raw[:].rearrange("p a c -> p (a c)").bitcast(I32), 0)
         tab_bytes = keep.tile([P, T], U8, name="tab_bytes", align_bytes=ALIGN)
         nc.sync.dma_start(
@@ -61,16 +61,14 @@ def tile_list_syntax_edge_types_kernel(
                 out=w4_bytes_raw[r:P:32, :, :].bitcast(I32),
                 in_=w4_scales[:, r:16:4, :].rearrange("a q c -> q a c").bitcast(I32),
             )
-        w4_raw = early.tile([P, PASSES, H], U16, name="w4_raw", offset=19456, align_bytes=ALIGN)
-        nc.sync.dma_start(out=w4_raw[:].bitcast(I32), in_=w4_words.rearrange("a p c -> p a c").bitcast(I32))
         tab = [
             shared.tile([P, T], I32, name="tab0", offset=0, align_bytes=ALIGN),
             keep.tile([P, T], I32, name="tab1", tag="window1", align_bytes=ALIGN),
         ]
         for a in range(PASSES):
             nc.sync.dma_start(out=tab[a][:], in_=tab_words[a].rearrange("p t i -> p (t i)").bitcast(I32))
-        idx2 = lists.tile([P, M // LANES], U16, name="idx2")
-        nc.sync.dma_start(idx2[:], offs2)
+        w4_raw = keep.tile([P, PASSES, H], U16, name="w4_raw", align_bytes=ALIGN)
+        nc.sync.dma_start(out=w4_raw[:].bitcast(I32), in_=w4_words.rearrange("a p c -> p a c").bitcast(I32))
         v_bytes = [keep.tile([P, S], U8, name="v_bytes%d" % a, align_bytes=ALIGN) for a in range(PASSES)]
         nc.vector.memset(v_bytes[0][:].bitcast(I32), 0)
         nc.gpsimd.memset(v_bytes[1][:].bitcast(I32), 0)
@@ -78,7 +76,7 @@ def tile_list_syntax_edge_types_kernel(
         gains = keep.tile([P, PACK], F32, name="gains")
         nc.gpsimd.dma_start(out=gains[:], in_=gain.rearrange("(p i) -> p i", i=PACK))
 
-        picked = keep.tile([P, S], U8, name="picked", align_bytes=ALIGN)
+        picked = shared.tile([P, S], U8, name="picked", offset=4 * T, align_bytes=ALIGN)
         nc.vector.tensor_copy(out=picked[:], in_=tab_bytes[:].indirect(idx[:]))
 
         def move_scales(a):
@@ -89,10 +87,17 @@ def tile_list_syntax_edge_types_kernel(
                 )
 
         move_scales(0)
+        w4_bytes = keep.tile([P, PASSES, H], U8, name="w4_bytes", align_bytes=ALIGN)
+        nc.vector.tensor_copy(
+            out=w4_bytes[:].rearrange("p a (i m) -> p a i m", i=PACK),
+            in_=w4_bytes_raw[:].rearrange("p a (m i) -> p a i m", i=PACK),
+        )
+        warm = spare.tile([P, 1], F32, name="warm")
+        nc.scalar.activation(out=warm[:], in_=gains[:, 0:1], func=ACT.Sigmoid)
         w4_codes = []
         for i in range(PACK):
             codes = dealt.tile([P, PASSES, P], U16, name="w4_codes%d" % i, offset=1024 * i, align_bytes=ALIGN)
-            nc.vector.tensor_copy(out=codes[:], in_=w4_raw[:].rearrange("p a (m i) -> p a i m", i=PACK)[:, :, i, :])
+            nc.scalar.copy(out=codes[:], in_=w4_raw[:].rearrange("p a (m i) -> p a i m", i=PACK)[:, :, i, :])
             w4_codes.append(codes)
         wg_raw = [early.tile([P, PACK, H], F32, name="wg_raw%d" % a, offset=12288 + 8192 * a, align_bytes=ALIGN) for a in range(PASSES)]
         for a in range(PASSES):
@@ -111,15 +116,13 @@ def tile_list_syntax_edge_types_kernel(
 
         v0 = keep.tile([P, S], U32, name="v0", align_bytes=ALIGN)
         nc.vector.tensor_copy(out=v0[:], in_=tab[0][:].bitcast(U32).indirect(idx[:]))
-        w4_bytes = keep.tile([P, PASSES, H], U8, name="w4_bytes", align_bytes=ALIGN)
-        nc.vector.tensor_copy(
-            out=w4_bytes[:].rearrange("p a (i m) -> p a i m", i=PACK),
-            in_=w4_bytes_raw[:].rearrange("p a (m i) -> p a i m", i=PACK),
-        )
         v1 = [look_up(c) for c in range(CHUNKS)]
 
         def round_wg(a):
-            dst = keep.tile([P, PACK, P, PACK], BF16, name="wg_bf%d" % a, tag="wg_bf%d" % a, align_bytes=ALIGN)
+            if a == 0:
+                dst = shared.tile([P, PACK, P, PACK], BF16, name="wg_bf0", offset=0, align_bytes=ALIGN)
+            else:
+                dst = keep.tile([P, PACK, P, PACK], BF16, name="wg_bf1", tag="wg_bf1", align_bytes=ALIGN)
             o = dst[:].rearrange("p i m j -> p m i j")
             s = wg_raw[a][:].rearrange("p j (m i) -> p m i j", i=PACK)
             split = SPLITS[a]
@@ -134,10 +137,10 @@ def tile_list_syntax_edge_types_kernel(
                 nc.vector.tensor_copy(out=o_run[:, split:], in_=s_run[:, split:])
             return dst
 
-        warm = spare.tile([P, 1], F32, name="warm")
-        nc.scalar.activation(out=warm[:], in_=wg_raw[0][:, 0, 0:1], func=ACT.Sigmoid)
         wg_bf = [round_wg(a) for a in range(PASSES)]
 
+        idx2 = lists.tile([P, M // LANES], U16, name="idx2")
+        nc.sync.dma_start(idx2[:], offs2)
         weights = early.tile([P, M], F32, name="weights", offset=16384, align_bytes=ALIGN)
         nc.sync.dma_start(out=weights[:], in_=wgt)
         sites = early.tile([P, PACK, M], F32, name="sites", offset=0, align_bytes=ALIGN)
@@ -158,7 +161,7 @@ def tile_list_syntax_edge_types_kernel(
                 rows = slice((i - lo) * P, (i - lo + 1) * P)
                 wg_tiles[(a, i)] = (codes[:, rows].bitcast(FP8X4), scales[:, rows])
 
-        quantize_wg(0, 0, 1, (early, 28672))
+        quantize_wg(0, 0, 1, (shared, 4 * T))
         quantize_wg(1, 0, 1, (early, 29184))
         quantize_wg(0, 1, 2, (early, 20480))
         quantize_wg(1, 1, 3, (relay, 0))
@@ -217,9 +220,11 @@ def tile_list_syntax_edge_types_kernel(
         def add_site(engine, y, x, i, lo, hi):
             engine.tensor_tensor(out=y, in0=x, in1=sites[:, i, lo:hi], op=ALU.add)
 
+        last = PACK - 1
+
         def scale(u, i, t):
             dst = z[u][:, i // 2, :, i % 2]
-            if i < 2:
+            if i < last:
                 nc.scalar.activation(out=dst, in_=t, func=ACT.Copy, scale=gains[:, i : i + 1])
             else:
                 nc.vector.tensor_scalar(out=dst, in0=t, scalar1=gains[:, i : i + 1], scalar2=None, op0=ALU.mult)
@@ -256,7 +261,6 @@ def tile_list_syntax_edge_types_kernel(
                 rows = out[b * PER_BANK * P : (b + 1) * PER_BANK * P, u * SITES : (u + 1) * SITES]
                 nc.sync.dma_start(out=rows.rearrange("(e p) m -> p e m", p=P), in_=result[:])
 
-        last = PACK - 1
         half = CHUNKS // 2
         contents = [None if c == half else product(0, c, False, passes=[0]) for c in range(CHUNKS)]
         for c in range(CHUNKS):
@@ -281,7 +285,9 @@ def tile_list_syntax_edge_types_kernel(
                 for u in range(SITE_CHUNKS):
                     scale(u, i - 1, t[:, u * SITES : (u + 1) * SITES])
             if i == last:
-                nc.scalar.activation(out=xs[i - 1][:], in_=xs[i - 1][:], func=ACT.Tanh)
+                nc.scalar.activation(out=xs[i - 1][:, : 2 * SITES], in_=xs[i - 1][:, : 2 * SITES], func=ACT.Tanh)
+                for u in range(2):
+                    scale(u, i - 1, xs[i - 1][:, u * SITES : (u + 1) * SITES])
             if i < last:
                 contents = [product(i + 1, c, False) for c in range(CHUNKS)]
                 sigs = ahead
@@ -299,15 +305,20 @@ def tile_list_syntax_edge_types_kernel(
                 place = 2048 * (step - 2) if step >= 2 else 8192 + 1024 * step
                 x = tail.tile([P, SITES], F32, name="x_last%d" % step, offset=place, align_bytes=ALIGN)
                 pick(x[:], last, lo, hi)
-                scale(step, last - 1, xs[last - 1][:, lo:hi] if hi <= POOL_SITES else rest[:])
                 add_site(nc.vector, x[:], x[:], last, lo, hi)
-                nc.scalar.activation(out=x[:], in_=x[:], func=ACT.Tanh)
-                squashed.append(x)
+                t = tail.tile([P, SITES], F32, name="t_last%d" % step, offset=10240 + 1024 * step, align_bytes=ALIGN)
+                nc.scalar.activation(out=t[:], in_=x[:], func=ACT.Tanh)
+                squashed.append(t)
+            if step == 0:
+                late = tail.tile([P, SITES], F32, name="late", offset=8192, align_bytes=ALIGN)
+                nc.scalar.activation(out=late[:], in_=xs[last - 1][:, 2 * SITES :], func=ACT.Tanh)
+                scale(2, last - 1, late[:])
             if step == 1:
                 rest = dealt.tile([P, M - POOL_SITES], F32, name="rest2", offset=1024 * last, align_bytes=ALIGN)
                 pick(rest[:], last - 1, POOL_SITES, M)
                 add_site(nc.vector, rest[:], rest[:], last - 1, POOL_SITES, M)
                 nc.scalar.activation(out=rest[:], in_=rest[:], func=ACT.Tanh)
+                scale(SITE_CHUNKS - 1, last - 1, rest[:])
             if 1 <= step <= SITE_CHUNKS:
                 scale(step - 1, last, squashed[step - 1][:])
                 banks.append(scores(step - 1))

@@ -144,7 +144,9 @@ def tile_list_syntax_edge_types_kernel(
         weights = early.tile([P, M], F32, name="weights", offset=16384, align_bytes=ALIGN)
         nc.sync.dma_start(out=weights[:], in_=wgt)
         sites = early.tile([P, PACK, M], F32, name="sites", offset=0, align_bytes=ALIGN)
-        nc.sync.dma_start(out=sites[:], in_=site.rearrange("(p i) m -> p i m", i=PACK))
+        site_rows = site.rearrange("(p i) m -> p i m", i=PACK)
+        nc.sync.dma_start(out=sites[:, :1, :], in_=site_rows[:, :1, :])
+        nc.sync.dma_start(out=sites[:, 1:, :], in_=site_rows[:, 1:, :])
         wg_tiles = {}
 
         def quantize_wg(a, lo, hi, place):
@@ -253,7 +255,7 @@ def tile_list_syntax_edge_types_kernel(
 
         def store(u, banks):
             for b, acc in enumerate(banks):
-                result = ring.tile([P, PER_BANK, SITES], F32, name="result", bufs=8, align_bytes=ALIGN)
+                result = ring.tile([P, PER_BANK, SITES], F32, name="result", bufs=12, align_bytes=ALIGN)
                 if u == SITE_CHUNKS - 1 and b != 1:
                     nc.vector.tensor_copy(out=result[:], in_=acc[:])
                 else:

@@ -25,7 +25,7 @@ SITES = 256
 SITE_CHUNKS = M // SITES
 LANES = 16
 PER_BANK = BANK // SITES
-SPLITS = (72, 46)
+SPLITS = (64, 40)
 POOL_SITES = 768
 ALIGN = 256
 
@@ -163,11 +163,9 @@ def tile_list_syntax_edge_types_kernel(
                 rows = slice((i - lo) * P, (i - lo + 1) * P)
                 wg_tiles[(a, i)] = (codes[:, rows].bitcast(FP8X4), scales[:, rows])
 
-        quantize_wg(0, 0, 1, (shared, 4 * T))
+        quantize_wg(0, 0, 4, (shared, 4 * T))
         quantize_wg(1, 0, 1, (early, 29184))
-        quantize_wg(0, 1, 2, (early, 20480))
         quantize_wg(1, 1, 3, (relay, 0))
-        quantize_wg(0, 2, 4, (early, 20992))
         quantize_wg(1, 3, 4, (relay, 4096))
         w8_bytes = keep.tile([P, N], U8, name="w8_bytes", tag="wg_bf1", align_bytes=ALIGN)
         nc.gpsimd.memset(w8_bytes[:].bitcast(I32), 0)
@@ -180,18 +178,18 @@ def tile_list_syntax_edge_types_kernel(
         w8_codes = keep.tile([P, N], I32, name="w8_codes", tag="window1", align_bytes=ALIGN)
         nc.sync.dma_start(out=w8_codes[:], in_=w8_words[0].rearrange("p c i -> p (c i)").bitcast(I32))
 
-        def table(a, c):
-            span = slice(c * BANK, (c + 1) * BANK)
+        def table(a, c, lo, hi):
+            span = slice(c * BANK + lo, c * BANK + hi)
             if a == 0:
                 return v0[:, span].bitcast(FP8X4), v_bytes[0][:, span]
-            return v1[c][:].bitcast(FP8X4), v_bytes[1][:, span]
+            return v1[c][:, lo:hi].bitcast(FP8X4), v_bytes[1][:, span]
 
-        def product(i, c, gate, acc=None, passes=range(PASSES), first=0):
+        def product(i, c, gate, acc=None, passes=range(PASSES), first=0, lo=0, hi=BANK):
             if acc is None:
-                acc = psum.tile([P, BANK], F32, name="acc", tag="gate" if gate else "content")
+                acc = psum.tile([P, hi - lo], F32, name="acc", tag="gate" if gate else "content")
             rows = slice(i * P, (i + 1) * P)
             for a in passes:
-                codes, scales = table(a, c)
+                codes, scales = table(a, c, lo, hi)
                 if gate:
                     lhs, lhs_scale = wg_tiles[(a, i)]
                 else:
@@ -204,13 +202,17 @@ def tile_list_syntax_edge_types_kernel(
 
         h = [keep.tile([P, S], F32, name="h%d" % i, align_bytes=ALIGN) for i in range(PACK)]
 
-        def sigmoid(acc):
-            sig = ring.tile([P, BANK], F32, name="sig", bufs=8, align_bytes=ALIGN)
-            nc.scalar.activation(out=sig[:], in_=acc[:], func=ACT.Sigmoid)
-            return sig
+        def sigmoid(acc, lo=0, hi=BANK, sig=None):
+            if sig is None:
+                sig = ring.tile([P, hi - lo], F32, name="sig", bufs=8, align_bytes=ALIGN)
+            nc.scalar.activation(out=sig[:], in_=acc, func=ACT.Sigmoid)
+            return lo, hi, sig
 
-        def gated(i, c, content, sig):
-            nc.vector.tensor_tensor(out=h[i][:, c * BANK : (c + 1) * BANK], in0=content[:], in1=sig[:], op=ALU.mult)
+        def gated(i, c, content, pieces):
+            for lo, hi, sig in pieces:
+                nc.vector.tensor_tensor(
+                    out=h[i][:, c * BANK + lo : c * BANK + hi], in0=content[:, lo:hi], in1=sig[:], op=ALU.mult
+                )
 
         z = [keep.tile([P, 2, SITES, 2], BF16, name="z%d" % u, align_bytes=ALIGN) for u in range(SITE_CHUNKS)]
 
@@ -270,12 +272,18 @@ def tile_list_syntax_edge_types_kernel(
                 contents[c] = product(0, c, False, passes=[1, 0], first=1)
             else:
                 product(0, c, False, contents[c], [1])
-        gates = [product(0, c, True, passes=[0]) for c in range(half)]
-        sigs = [sigmoid(product(0, c, True, gates[c], [1])) for c in range(half)]
-        sigs.extend(sigmoid(product(0, c, True, passes=[1, 0], first=1)) for c in range(half, CHUNKS))
+        cuts = [(0, BANK // 2), (BANK // 2, BANK)]
+        opened = [product(0, 0, True, passes=[0], lo=lo, hi=hi) for lo, hi in cuts]
+        second = product(0, 1, True, passes=[0])
+        third = product(0, 2, True, passes=[0])
+        sigs = [[sigmoid(product(0, 0, True, acc, [1], lo=lo, hi=hi)[:], lo, hi) for acc, (lo, hi) in zip(opened, cuts)]]
+        sigs.append([sigmoid(product(0, 1, True, second, [1])[:])])
+        sigs.append([sigmoid(product(0, 2, True, third, [1])[:])])
+        fourth = product(0, 3, True)
+        sigs.append([sigmoid(fourth[:, lo:hi], lo, hi) for lo, hi in cuts])
         xs = []
         for i in range(PACK):
-            ahead = [sigmoid(product(i + 1, c, True)) for c in range(CHUNKS)] if i < last else []
+            ahead = [[sigmoid(product(i + 1, c, True)[:])] for c in range(CHUNKS)] if i < last else []
             for c in range(CHUNKS):
                 gated(i, c, contents[c], sigs[c])
             if 1 <= i < last:

@@ -25,7 +25,7 @@ SITES = 256
 SITE_CHUNKS = M // SITES
 LANES = 16
 PER_BANK = BANK // SITES
-SPLITS = (64, 40)
+SPLITS = (72, 44)
 POOL_SITES = 768
 ALIGN = 256
 
@@ -43,6 +43,7 @@ def tile_list_syntax_edge_types_kernel(
         relay = ctx.enter_context(tc.tile_pool(name="relay", bufs=1))
         dealt = ctx.enter_context(tc.tile_pool(name="dealt", bufs=1))
         ring = ctx.enter_context(tc.tile_pool(name="ring", bufs=4))
+        hold = ctx.enter_context(tc.tile_pool(name="hold", bufs=1))
         spare = ctx.enter_context(tc.tile_pool(name="spare", bufs=1))
         psum = ctx.enter_context(tc.psum_pool(name="psum", bufs=4))
 
@@ -56,17 +57,17 @@ def tile_list_syntax_edge_types_kernel(
         nc.vector.memset(tab_bytes[64:128, :].bitcast(I32), 0)
         idx = lists.tile([P, S // LANES], U16, name="idx")
         nc.sync.dma_start(idx[:], offs)
+        tab = [
+            shared.tile([P, T], I32, name="tab0", offset=0, align_bytes=ALIGN),
+            keep.tile([P, T], I32, name="tab1", tag="window1", align_bytes=ALIGN),
+        ]
+        nc.sync.dma_start(out=tab[0][:], in_=tab_words[0].rearrange("p t i -> p (t i)").bitcast(I32))
         for r in range(4):
             nc.sync.dma_start(
                 out=w4_bytes_raw[r:P:32, :, :].bitcast(I32),
                 in_=w4_scales[:, r:16:4, :].rearrange("a q c -> q a c").bitcast(I32),
             )
-        tab = [
-            shared.tile([P, T], I32, name="tab0", offset=0, align_bytes=ALIGN),
-            keep.tile([P, T], I32, name="tab1", tag="window1", align_bytes=ALIGN),
-        ]
-        for a in range(PASSES):
-            nc.sync.dma_start(out=tab[a][:], in_=tab_words[a].rearrange("p t i -> p (t i)").bitcast(I32))
+        nc.sync.dma_start(out=tab[1][:], in_=tab_words[1].rearrange("p t i -> p (t i)").bitcast(I32))
         w4_raw = keep.tile([P, PASSES, H], U16, name="w4_raw", align_bytes=ALIGN)
         nc.sync.dma_start(out=w4_raw[:].bitcast(I32), in_=w4_words.rearrange("a p c -> p a c").bitcast(I32))
         v_bytes = [keep.tile([P, S], U8, name="v_bytes%d" % a, align_bytes=ALIGN) for a in range(PASSES)]
@@ -88,7 +89,7 @@ def tile_list_syntax_edge_types_kernel(
 
         move_scales(0)
         w4_bytes = keep.tile([P, PASSES, H], U8, name="w4_bytes", align_bytes=ALIGN)
-        nc.vector.tensor_copy(
+        nc.gpsimd.tensor_copy(
             out=w4_bytes[:].rearrange("p a (i m) -> p a i m", i=PACK),
             in_=w4_bytes_raw[:].rearrange("p a (m i) -> p a i m", i=PACK),
         )
@@ -149,11 +150,14 @@ def tile_list_syntax_edge_types_kernel(
         nc.sync.dma_start(out=sites[:, 1:, :], in_=site_rows[:, 1:, :])
         wg_tiles = {}
 
-        def quantize_wg(a, lo, hi, place):
+        def quantize_wg(a, lo, hi, place, late=None):
             width = (hi - lo) * P
             pool, offset = place
             codes = pool.tile([P, width], U32, name="wg_codes%d_%d" % (a, lo), offset=offset, align_bytes=ALIGN)
-            scales = keep.tile([P, width], U8, name="wg_bytes%d_%d" % (a, lo), align_bytes=ALIGN)
+            if late is None:
+                scales = keep.tile([P, width], U8, name="wg_bytes%d_%d" % (a, lo), align_bytes=ALIGN)
+            else:
+                scales = late.tile([P, width], U8, name="wg_bytes%d_%d" % (a, lo), offset=0, align_bytes=ALIGN)
             nc.vector.quantize_mx(
                 out=codes[:].bitcast(FP8X4),
                 scales=scales[:],
@@ -163,21 +167,10 @@ def tile_list_syntax_edge_types_kernel(
                 rows = slice((i - lo) * P, (i - lo + 1) * P)
                 wg_tiles[(a, i)] = (codes[:, rows].bitcast(FP8X4), scales[:, rows])
 
-        quantize_wg(0, 0, 4, (shared, 4 * T))
+        quantize_wg(0, 0, 2, (shared, 4 * T))
         quantize_wg(1, 0, 1, (early, 29184))
         quantize_wg(1, 1, 3, (relay, 0))
-        quantize_wg(1, 3, 4, (relay, 4096))
-        w8_bytes = keep.tile([P, N], U8, name="w8_bytes", tag="wg_bf1", align_bytes=ALIGN)
-        nc.gpsimd.memset(w8_bytes[:].bitcast(I32), 0)
-        for q in range(4):
-            nc.sync.dma_start(
-                out=w8_bytes[32 * q : 32 * q + 4, :].bitcast(I32),
-                in_=w8_scales[0, 4 * q : 4 * q + 4, :].bitcast(I32),
-            )
-
-        w8_codes = keep.tile([P, N], I32, name="w8_codes", tag="window1", align_bytes=ALIGN)
-        nc.sync.dma_start(out=w8_codes[:], in_=w8_words[0].rearrange("p c i -> p (c i)").bitcast(I32))
-
+        quantize_wg(0, 2, 4, (early, 20992))
         def table(a, c, lo, hi):
             span = slice(c * BANK + lo, c * BANK + hi)
             if a == 0:
@@ -278,14 +271,26 @@ def tile_list_syntax_edge_types_kernel(
         third = product(0, 2, True, passes=[0])
         sigs = [[sigmoid(product(0, 0, True, acc, [1], lo=lo, hi=hi)[:], lo, hi) for acc, (lo, hi) in zip(opened, cuts)]]
         sigs.append([sigmoid(product(0, 1, True, second, [1])[:])])
-        sigs.append([sigmoid(product(0, 2, True, third, [1])[:])])
-        fourth = product(0, 3, True)
-        sigs.append([sigmoid(fourth[:, lo:hi], lo, hi) for lo, hi in cuts])
+        held = hold.tile([P, BANK], F32, name="held", offset=0, align_bytes=ALIGN)
+        sigs.append([sigmoid(product(0, 2, True, third, [1])[:], sig=held)])
+        sigs.append([sigmoid(product(0, 3, True)[:])])
         xs = []
         for i in range(PACK):
             ahead = [[sigmoid(product(i + 1, c, True)[:])] for c in range(CHUNKS)] if i < last else []
             for c in range(CHUNKS):
                 gated(i, c, contents[c], sigs[c])
+            if i == 0:
+                quantize_wg(1, 3, 4, (relay, 4096), hold)
+                w8_bytes = keep.tile([P, N], U8, name="w8_bytes", tag="wg_bf1", align_bytes=ALIGN)
+                nc.gpsimd.memset(w8_bytes[:].bitcast(I32), 0)
+                for q in range(4):
+                    nc.sync.dma_start(
+                        out=w8_bytes[32 * q : 32 * q + 4, :].bitcast(I32),
+                        in_=w8_scales[0, 4 * q : 4 * q + 4, :].bitcast(I32),
+                    )
+
+                w8_codes = keep.tile([P, N], I32, name="w8_codes", tag="window1", align_bytes=ALIGN)
+                nc.sync.dma_start(out=w8_codes[:], in_=w8_words[0].rearrange("p c i -> p (c i)").bitcast(I32))
             if 1 <= i < last:
                 rest = dealt.tile([P, M - POOL_SITES], F32, name="rest%d" % (i - 1), offset=1024 * i, align_bytes=ALIGN)
                 add_site(nc.vector, rest[:], xs[i - 1][:, POOL_SITES:], i - 1, POOL_SITES, M)

from contextlib import ExitStack

import concourse.mybir as mybir

T, S, M, K, H, N = 4096, 2048, 1024, 1024, 512, 768
FLOPS = 2 * (2 * K * H * S + H * N * M)

F32 = mybir.dt.float32
BF16 = mybir.dt.bfloat16
I32 = mybir.dt.int32
U32 = mybir.dt.uint32
U16 = mybir.dt.uint16
U8 = mybir.dt.uint8
FP8X4 = mybir.dt.float8_e4m3fn_x4
FP4X4 = mybir.dt.float4_e2m1fn_x4
ACT = mybir.ActivationFunctionType
ALU = mybir.AluOpType

P = 128
PACK = 4
PASSES = K // (P * PACK)
BANK = 512
CHUNKS = S // BANK
SITES = 256
SITE_CHUNKS = M // SITES
LANES = 16
PER_BANK = BANK // SITES
SPLITS = (72, 44)
POOL_SITES = 768
ALIGN = 256


def tile_list_syntax_edge_types_kernel(
    tc, tab_words, tab_scales, offs, w4_words, w4_scales, wg, offs2, wgt, site, gain, w8_words, w8_scales, out
):
    nc = tc.nc
    with ExitStack() as ctx:
        lists = ctx.enter_context(tc.tile_pool(name="lists", bufs=1))
        keep = ctx.enter_context(tc.tile_pool(name="keep", bufs=1))
        shared = ctx.enter_context(tc.tile_pool(name="shared", bufs=1))
        early = ctx.enter_context(tc.tile_pool(name="early", bufs=1))
        tail = ctx.enter_context(tc.tile_pool(name="tail", bufs=1))
        relay = ctx.enter_context(tc.tile_pool(name="relay", bufs=1))
        dealt = ctx.enter_context(tc.tile_pool(name="dealt", bufs=1))
        ring = ctx.enter_context(tc.tile_pool(name="ring", bufs=4))
        hold = ctx.enter_context(tc.tile_pool(name="hold", bufs=1))
        spare = ctx.enter_context(tc.tile_pool(name="spare", bufs=1))
        psum = ctx.enter_context(tc.psum_pool(name="psum", bufs=4))

        w4_bytes_raw = early.tile([P, PASSES, H], U8, name="w4_bytes_raw", offset=19968, align_bytes=ALIGN)
        nc.gpsimd.memset(w4_bytes_raw[:].rearrange("p a c -> p (a c)").bitcast(I32), 0)
        tab_bytes = keep.tile([P, T], U8, name="tab_bytes", align_bytes=ALIGN)
        nc.sync.dma_start(
            out=tab_bytes[0:32, :].bitcast(I32), in_=tab_scales.rearrange("a q t -> (a q) t").bitcast(I32)
        )
        nc.gpsimd.memset(tab_bytes[32:64, :].bitcast(I32), 0)
        nc.vector.memset(tab_bytes[64:128, :].bitcast(I32), 0)
        idx = lists.tile([P, S // LANES], U16, name="idx")
        nc.sync.dma_start(idx[:], offs)
        tab = [
            shared.tile([P, T], I32, name="tab0", offset=0, align_bytes=ALIGN),
            keep.tile([P, T], I32, name="tab1", tag="window1", align_bytes=ALIGN),
        ]
        nc.sync.dma_start(out=tab[0][:], in_=tab_words[0].rearrange("p t i -> p (t i)").bitcast(I32))
        for r in range(4):
            nc.sync.dma_start(
                out=w4_bytes_raw[r:P:32, :, :].bitcast(I32),
                in_=w4_scales[:, r:16:4, :].rearrange("a q c -> q a c").bitcast(I32),
            )
        nc.sync.dma_start(out=tab[1][:], in_=tab_words[1].rearrange("p t i -> p (t i)").bitcast(I32))
        w4_raw = keep.tile([P, PASSES, H], U16, name="w4_raw", align_bytes=ALIGN)
        nc.sync.dma_start(out=w4_raw[:].bitcast(I32), in_=w4_words.rearrange("a p c -> p a c").bitcast(I32))
        v_bytes = [keep.tile([P, S], U8, name="v_bytes%d" % a, align_bytes=ALIGN) for a in range(PASSES)]
        nc.vector.memset(v_bytes[0][:].bitcast(I32), 0)
        nc.gpsimd.memset(v_bytes[1][:].bitcast(I32), 0)

        gains = keep.tile([P, PACK], F32, name="gains")
        nc.gpsimd.dma_start(out=gains[:], in_=gain.rearrange("(p i) -> p i", i=PACK))

        picked = shared.tile([P, S], U8, name="picked", offset=4 * T, align_bytes=ALIGN)
        nc.vector.tensor_copy(out=picked[:], in_=tab_bytes[:].indirect(idx[:]))

        def move_scales(a):
            for r in range(4):
                nc.sync.dma_start(
                    out=v_bytes[a][r:P:32, :].bitcast(I32),
                    in_=picked[16 * a + r : 16 * a + 16 : 4, :].bitcast(I32),
                )

        move_scales(0)
        w4_bytes = keep.tile([P, PASSES, H], U8, name="w4_bytes", align_bytes=ALIGN)
        nc.gpsimd.tensor_copy(
            out=w4_bytes[:].rearrange("p a (i m) -> p a i m", i=PACK),
            in_=w4_bytes_raw[:].rearrange("p a (m i) -> p a i m", i=PACK),
        )
        warm = spare.tile([P, 1], F32, name="warm")
        nc.scalar.activation(out=warm[:], in_=gains[:, 0:1], func=ACT.Sigmoid)
        w4_codes = []
        for i in range(PACK):
            codes = dealt.tile([P, PASSES, P], U16, name="w4_codes%d" % i, offset=1024 * i, align_bytes=ALIGN)
            nc.scalar.copy(out=codes[:], in_=w4_raw[:].rearrange("p a (m i) -> p a i m", i=PACK)[:, :, i, :])
            w4_codes.append(codes)
        wg_raw = [early.tile([P, PACK, H], F32, name="wg_raw%d" % a, offset=12288 + 8192 * a, align_bytes=ALIGN) for a in range(PASSES)]
        for a in range(PASSES):
            nc.sync.dma_start(
                out=wg_raw[a][:], in_=wg[a * P * PACK : (a + 1) * P * PACK, :].rearrange("(p j) c -> p j c", j=PACK)
            )
            if a == 0:
                move_scales(1)

        cols = BANK // LANES

        def look_up(c):
            piece = keep.tile([P, BANK], U32, name="v1_%d" % c, tag="v1_%d" % c, align_bytes=ALIGN)
            nc.vector.tensor_copy(out=piece[:], in_=tab[1][:].bitcast(U32).indirect(idx[:, c * cols : (c + 1) * cols]))
            return piece

        v0 = keep.tile([P, S], U32, name="v0", align_bytes=ALIGN)
        nc.vector.tensor_copy(out=v0[:], in_=tab[0][:].bitcast(U32).indirect(idx[:]))
        v1 = [look_up(c) for c in range(CHUNKS)]

        def round_wg(a):
            if a == 0:
                dst = shared.tile([P, PACK, P, PACK], BF16, name="wg_bf0", offset=0, align_bytes=ALIGN)
            else:
                dst = keep.tile([P, PACK, P, PACK], BF16, name="wg_bf1", tag="wg_bf1", align_bytes=ALIGN)
            o = dst[:].rearrange("p i m j -> p m i j")
            s = wg_raw[a][:].rearrange("p j (m i) -> p m i j", i=PACK)
            split = SPLITS[a]
            o_run = dst[:].rearrange("p i m j -> p m j i")
            s_run = wg_raw[a][:].rearrange("p j (m i) -> p m j i", i=PACK)
            nc.scalar.copy(out=o_run[:, :split], in_=s_run[:, :split])
            if a == 0:
                nc.gpsimd.tensor_scalar(
                    out=o[:, split:], in0=s[:, split:], scalar1=1.0, scalar2=0.0, op0=ALU.mult, op1=ALU.add
                )
            else:
                nc.vector.tensor_copy(out=o_run[:, split:], in_=s_run[:, split:])
            return dst

        wg_bf = [round_wg(a) for a in range(PASSES)]

        idx2 = lists.tile([P, M // LANES], U16, name="idx2")
        nc.sync.dma_start(idx2[:], offs2)
        weights = early.tile([P, M], F32, name="weights", offset=16384, align_bytes=ALIGN)
        nc.sync.dma_start(out=weights[:], in_=wgt)
        sites = early.tile([P, PACK, M], F32, name="sites", offset=0, align_bytes=ALIGN)
        site_rows = site.rearrange("(p i) m -> p i m", i=PACK)
        nc.sync.dma_start(out=sites[:, :1, :], in_=site_rows[:, :1, :])
        nc.sync.dma_start(out=sites[:, 1:, :], in_=site_rows[:, 1:, :])
        wg_tiles = {}

        def quantize_wg(a, lo, hi, place, late=None):
            width = (hi - lo) * P
            pool, offset = place
            codes = pool.tile([P, width], U32, name="wg_codes%d_%d" % (a, lo), offset=offset, align_bytes=ALIGN)
            if late is None:
                scales = keep.tile([P, width], U8, name="wg_bytes%d_%d" % (a, lo), align_bytes=ALIGN)
            else:
                scales = late.tile([P, width], U8, name="wg_bytes%d_%d" % (a, lo), offset=0, align_bytes=ALIGN)
            nc.vector.quantize_mx(
                out=codes[:].bitcast(FP8X4),
                scales=scales[:],
                in_=wg_bf[a][:, lo:hi].rearrange("p i m j -> p (i m j)"),
            )
            for i in range(lo, hi):
                rows = slice((i - lo) * P, (i - lo + 1) * P)
                wg_tiles[(a, i)] = (codes[:, rows].bitcast(FP8X4), scales[:, rows])

        quantize_wg(0, 0, 2, (shared, 4 * T))
        quantize_wg(1, 0, 1, (early, 29184))
        quantize_wg(1, 1, 3, (relay, 0))
        quantize_wg(0, 2, 4, (early, 20992))
        def table(a, c, lo, hi):
            span = slice(c * BANK + lo, c * BANK + hi)
            if a == 0:
                return v0[:, span].bitcast(FP8X4), v_bytes[0][:, span]
            return v1[c][:, lo:hi].bitcast(FP8X4), v_bytes[1][:, span]

        def product(i, c, gate, acc=None, passes=range(PASSES), first=0, lo=0, hi=BANK):
            if acc is None:
                acc = psum.tile([P, hi - lo], F32, name="acc", tag="gate" if gate else "content")
            rows = slice(i * P, (i + 1) * P)
            for a in passes:
                codes, scales = table(a, c, lo, hi)
                if gate:
                    lhs, lhs_scale = wg_tiles[(a, i)]
                else:
                    lhs, lhs_scale = w4_codes[i][:, a, :].bitcast(FP4X4), w4_bytes[:, a, rows]
                nc.tensor.matmul_mx(
                    out=acc[:], lhsT=lhs, lhsT_scale=lhs_scale, rhs=codes, rhs_scale=scales,
                    start=(a == first), stop=(a != first),
                )
            return acc

        h = [keep.tile([P, S], F32, name="h%d" % i, align_bytes=ALIGN) for i in range(PACK)]

        def sigmoid(acc, lo=0, hi=BANK, sig=None):
            if sig is None:
                sig = ring.tile([P, hi - lo], F32, name="sig", bufs=8, align_bytes=ALIGN)
            nc.scalar.activation(out=sig[:], in_=acc, func=ACT.Sigmoid)
            return lo, hi, sig

        def gated(i, c, content, pieces):
            for lo, hi, sig in pieces:
                nc.vector.tensor_tensor(
                    out=h[i][:, c * BANK + lo : c * BANK + hi], in0=content[:, lo:hi], in1=sig[:], op=ALU.mult
                )

        z = [keep.tile([P, 2, SITES, 2], BF16, name="z%d" % u, align_bytes=ALIGN) for u in range(SITE_CHUNKS)]

        def pick(x, i, lo, hi):
            nc.vector.tensor_tensor(
                out=x, in0=h[i][:].indirect(idx2[:, lo // LANES : hi // LANES]), in1=weights[:, lo:hi], op=ALU.mult
            )

        def add_site(engine, y, x, i, lo, hi):
            engine.tensor_tensor(out=y, in0=x, in1=sites[:, i, lo:hi], op=ALU.add)

        last = PACK - 1

        def scale(u, i, t):
            dst = z[u][:, i // 2, :, i % 2]
            if i < last:
                nc.scalar.activation(out=dst, in_=t, func=ACT.Copy, scale=gains[:, i : i + 1])
            else:
                nc.vector.tensor_scalar(out=dst, in0=t, scalar1=gains[:, i : i + 1], scalar2=None, op0=ALU.mult)

        def scores(u):
            woven = tail.tile([P, SITES, PACK], BF16, name="woven%d" % u, offset=2048 * u, align_bytes=ALIGN)
            nc.vector.tensor_copy(
                out=woven[:].bitcast(F32), in_=z[u][:].rearrange("p a m e -> p a (m e)").bitcast(F32).rearrange("p a m -> p m a")
            )
            z_codes = ring.tile([P, SITES], U32, name="z_codes", bufs=2, align_bytes=ALIGN)
            z_bytes = ring.tile([P, SITES], U8, name="z_bytes", bufs=2, align_bytes=ALIGN)
            nc.vector.quantize_mx(
                out=z_codes[:].bitcast(FP8X4), scales=z_bytes[:], in_=woven[:].rearrange("p m i -> p (m i)")
            )
            banks = []
            for b in range(N // P // PER_BANK):
                acc = psum.tile([P, PER_BANK, SITES], F32, name="acc2", tag="gate" if (3 * u + b) % 8 < 4 else "content")
                for e in range(PER_BANK):
                    types = slice((b * PER_BANK + e) * P, (b * PER_BANK + e + 1) * P)
                    nc.tensor.matmul_mx(
                        out=acc[:, e, :], lhsT=w8_codes[:, types].bitcast(FP8X4), lhsT_scale=w8_bytes[:, types],
                        rhs=z_codes[:].bitcast(FP8X4), rhs_scale=z_bytes[:], start=True, stop=True,
                    )
                banks.append(acc)
            return banks

        def store(u, banks):
            for b, acc in enumerate(banks):
                result = ring.tile([P, PER_BANK, SITES], F32, name="result", bufs=12, align_bytes=ALIGN)
                if u == SITE_CHUNKS - 1 and b != 1:
                    nc.vector.tensor_copy(out=result[:], in_=acc[:])
                else:
                    nc.scalar.copy(out=result[:], in_=acc[:])
                rows = out[b * PER_BANK * P : (b + 1) * PER_BANK * P, u * SITES : (u + 1) * SITES]
                nc.sync.dma_start(out=rows.rearrange("(e p) m -> p e m", p=P), in_=result[:])

        half = CHUNKS // 2
        contents = [None if c == half else product(0, c, False, passes=[0]) for c in range(CHUNKS)]
        for c in range(CHUNKS):
            if c == half:
                contents[c] = product(0, c, False, passes=[1, 0], first=1)
            else:
                product(0, c, False, contents[c], [1])
        cuts = [(0, BANK // 2), (BANK // 2, BANK)]
        opened = [product(0, 0, True, passes=[0], lo=lo, hi=hi) for lo, hi in cuts]
        second = product(0, 1, True, passes=[0])
        third = product(0, 2, True, passes=[0])
        sigs = [[sigmoid(product(0, 0, True, acc, [1], lo=lo, hi=hi)[:], lo, hi) for acc, (lo, hi) in zip(opened, cuts)]]
        sigs.append([sigmoid(product(0, 1, True, second, [1])[:])])
        held = hold.tile([P, BANK], F32, name="held", offset=0, align_bytes=ALIGN)
        sigs.append([sigmoid(product(0, 2, True, third, [1])[:], sig=held)])
        sigs.append([sigmoid(product(0, 3, True)[:])])
        xs = []
        for i in range(PACK):
            ahead = [[sigmoid(product(i + 1, c, True)[:])] for c in range(CHUNKS)] if i < last else []
            for c in range(CHUNKS):
                gated(i, c, contents[c], sigs[c])
            if i == 0:
                quantize_wg(1, 3, 4, (relay, 4096), hold)
                w8_bytes = keep.tile([P, N], U8, name="w8_bytes", tag="wg_bf1", align_bytes=ALIGN)
                nc.gpsimd.memset(w8_bytes[:].bitcast(I32), 0)
                for q in range(4):
                    nc.sync.dma_start(
                        out=w8_bytes[32 * q : 32 * q + 4, :].bitcast(I32),
                        in_=w8_scales[0, 4 * q : 4 * q + 4, :].bitcast(I32),
                    )

                w8_codes = keep.tile([P, N], I32, name="w8_codes", tag="window1", align_bytes=ALIGN)
                nc.sync.dma_start(out=w8_codes[:], in_=w8_words[0].rearrange("p c i -> p (c i)").bitcast(I32))
            if 1 <= i < last:
                rest = dealt.tile([P, M - POOL_SITES], F32, name="rest%d" % (i - 1), offset=1024 * i, align_bytes=ALIGN)
                add_site(nc.vector, rest[:], xs[i - 1][:, POOL_SITES:], i - 1, POOL_SITES, M)
                t = relay.tile([P, M], F32, name="t%d" % (i - 1), offset=(i - 1) * 4096, align_bytes=ALIGN)
                nc.scalar.activation(out=t[:, :POOL_SITES], in_=xs[i - 1][:, :POOL_SITES], func=ACT.Tanh)
                nc.scalar.activation(out=t[:, POOL_SITES:], in_=rest[:], func=ACT.Tanh)
                for u in range(SITE_CHUNKS):
                    scale(u, i - 1, t[:, u * SITES : (u + 1) * SITES])
            if i == last:
                nc.scalar.activation(out=xs[i - 1][:, : 2 * SITES], in_=xs[i - 1][:, : 2 * SITES], func=ACT.Tanh)
                for u in range(2):
                    scale(u, i - 1, xs[i - 1][:, u * SITES : (u + 1) * SITES])
            if i < last:
                contents = [product(i + 1, c, False) for c in range(CHUNKS)]
                sigs = ahead
                width = M if i < last - 1 else POOL_SITES
                x = keep.tile([P, width], F32, name="x%d" % i, align_bytes=ALIGN)
                pick(x[:], i, 0, width)
                add_site(nc.gpsimd, x[:, :POOL_SITES], x[:, :POOL_SITES], i, 0, POOL_SITES)
                xs.append(x)

        squashed = []
        banks = []
        for step in range(SITE_CHUNKS + 3):
            if step < SITE_CHUNKS:
                lo, hi = step * SITES, (step + 1) * SITES
                place = 2048 * (step - 2) if step >= 2 else 8192 + 1024 * step
                x = tail.tile([P, SITES], F32, name="x_last%d" % step, offset=place, align_bytes=ALIGN)
                pick(x[:], last, lo, hi)
                add_site(nc.vector, x[:], x[:], last, lo, hi)
                t = tail.tile([P, SITES], F32, name="t_last%d" % step, offset=10240 + 1024 * step, align_bytes=ALIGN)
                nc.scalar.activation(out=t[:], in_=x[:], func=ACT.Tanh)
                squashed.append(t)
            if step == 0:
                late = tail.tile([P, SITES], F32, name="late", offset=8192, align_bytes=ALIGN)
                nc.scalar.activation(out=late[:], in_=xs[last - 1][:, 2 * SITES :], func=ACT.Tanh)
                scale(2, last - 1, late[:])
            if step == 1:
                rest = dealt.tile([P, M - POOL_SITES], F32, name="rest2", offset=1024 * last, align_bytes=ALIGN)
                pick(rest[:], last - 1, POOL_SITES, M)
                add_site(nc.vector, rest[:], rest[:], last - 1, POOL_SITES, M)
                nc.scalar.activation(out=rest[:], in_=rest[:], func=ACT.Tanh)
                scale(SITE_CHUNKS - 1, last - 1, rest[:])
            if 1 <= step <= SITE_CHUNKS:
                scale(step - 1, last, squashed[step - 1][:])
                banks.append(scores(step - 1))
            if 2 <= step <= SITE_CHUNKS + 1:
                store(step - 2, banks[step - 2])
